import numpy as np
import ml_dtypes


def mxq(x, axis, fmt="e4m3"):
    dtype, down = {"e4m3": (ml_dtypes.float8_e4m3fn, 7), "e5m2": (ml_dtypes.float8_e5m2, 14)}[fmt]
    v = np.moveaxis(np.asarray(x, np.float32).astype(ml_dtypes.bfloat16).astype(np.float64), axis, -1)
    blocks = v.reshape(v.shape[:-1] + (-1, 32))
    amax = np.abs(blocks).max(-1, keepdims=True)
    byte = np.maximum(np.where(amax > 0, np.frexp(amax)[1] - 1 + 127, 0) - down, 1)
    scale = np.exp2(byte - 127.0)
    codes = (blocks / scale).astype(np.float32).astype(dtype).astype(np.float64)
    return np.moveaxis((codes * scale).reshape(v.shape), -1, axis)


WIDE = False


def mx_kscale(k):
    if not WIDE:
        return np.ones(k)
    levels = np.array([18, -18])
    if k % 512:
        return np.exp2(np.random.permutation(np.resize(levels, k // 32))).repeat(32)
    a = np.empty((k // 512, 16))
    for p in range(k // 512):
        a[p, :8] = np.random.permutation(np.resize(levels, 8))
        for g in range(8):
            far = levels[np.abs(levels - a[p, g]) >= 10]
            a[p, g + 8] = far[np.random.randint(len(far))]
    return np.exp2(a.ravel()).repeat(32)


def f64(x):
    return np.asarray(x).astype(np.float64)


def striped(idx):
    return np.tile(np.asarray(idx).reshape(-1, 16).T, (8, 1)).astype(np.uint16)


def unstriped(offs):
    return offs[:16].T.reshape(-1).astype(np.int64)


B, N, T, D, R = 2, 512, 2048, 512, 512


def setup_inputs():
    n = np.random.standard_normal
    idx = np.random.permutation(T)[:B * N]
    s = mx_kscale(D)[:, None]
    u = np.ones(T)
    u[idx] = mx_kscale(B * N)
    r = np.random.uniform(0.5, 2.0, T) * u
    x = n((B, D, R))
    return {
        "xT": (x * s).astype(np.float32),
        "wT": (n((D, T)) * (1.00 / np.sqrt(D)) / s / r).astype(np.float32),
        "y": n((B, R, N)).astype(np.float32),
        "wt": (np.random.uniform(0.5, 1.5, (B, R, 1)) * 1.0 / np.sqrt(R)).astype(np.float32),
        "ts": np.tile(r, (128, 1)).astype(np.float32),
        "offs": striped(idx),
    }


def reference(xT, wT, y, wt, ts, offs):
    idx = unstriped(offs)
    pick = lambda x: x[:, idx].reshape(x.shape[0], B, N).transpose(1, 0, 2)
    w = pick(f64(wT))
    a = mxq(f64(xT), 1, "e4m3").transpose(0, 2, 1) @ mxq(w, 1, "e4m3")
    ts_ = pick(f64(ts))[:, :1, :]
    a = a * ts_
    g = f64(wt) * np.minimum(np.maximum(a - f64(y), -1.0), 1.0)
    g = g * ts_
    gx = mxq(g, 2, "e5m2") @ mxq(w, 2, "e4m3").transpose(0, 2, 1)
    return gx

@@ -1,0 +1,237 @@
+from contextlib import ExitStack
+
+import concourse.mybir as mybir
+from concourse.masks import make_identity
+
+B, N, T, D, R = 2, 512, 2048, 512, 512
+FLOPS = 2 * 2 * B * R * N * D
+
+F32 = mybir.dt.float32
+BF16 = mybir.dt.bfloat16
+U32 = mybir.dt.uint32
+U16 = mybir.dt.uint16
+U8 = mybir.dt.uint8
+E4M3 = mybir.dt.float8_e4m3fn_x4
+E5M2 = mybir.dt.float8_e5m2_x4
+ALU = mybir.AluOpType
+ACT = mybir.ActivationFunctionType
+
+P = 128
+PACK = 4
+LIST_COLS = N // 16
+
+
+def tile_attend_ghub_x_ts_kernel(tc, xT, wT, y, wt, ts, offs, out):
+    nc = tc.nc
+    with ExitStack() as ctx:
+        keep = ctx.enter_context(tc.tile_pool(name="keep", bufs=1))
+        ring = ctx.enter_context(tc.tile_pool(name="ring", bufs=3))
+        stage = ctx.enter_context(tc.tile_pool(name="stage", bufs=PACK))
+        psum = ctx.enter_context(tc.psum_pool(name="psum", bufs=2))
+
+        def held(shape, dtype, name):
+            return keep.tile(shape, dtype, name=name, align_bytes=64)
+
+        offsets = keep.tile([P, B * LIST_COLS], U16, name="offsets")
+        nc.sync.dma_start(offsets[:], offs)
+        ts_row = held([P, T], F32, "ts_row")
+        nc.sync.dma_start(ts_row[0:32, :], ts[0:32, :])
+        nc.gpsimd.memset(ts_row[32:64, :], 0.0)
+        nc.vector.memset(ts_row[64:P, :], 0.0)
+        wt_cols = held([P, B, PACK], F32, "wt_cols")
+        nc.scalar.dma_start(wt_cols[:], wt.rearrange("b (p c) o -> p b (c o)", c=PACK))
+        w_planes = wT.rearrange("(p j) t -> p j t", j=PACK)
+        table = []
+        for j in range(PACK):
+            table.append(stage.tile([P, T], F32, name="table", tag="staged"))
+            nc.sync.dma_start(table[j][:], w_planes[:, j, :])
+        x_raw, y_raw = [], []
+
+        def load_group(b):
+            y_raw.append(stage.tile([P, PACK, N], F32, name="y_raw", tag="staged"))
+            nc.sync.dma_start(y_raw[b][:], y[b].rearrange("(p c) n -> p c n", c=PACK))
+            x_raw.append(stage.tile([P, PACK, R], F32, name="x_raw", tag="staged"))
+            nc.sync.dma_start(x_raw[b][:], xT[b].rearrange("(p j) r -> p j r", j=PACK))
+
+        identity = held([P, P], F32, "identity")
+        make_identity(nc, identity[:])
+
+        def group_offsets(b):
+            return offsets[:, b * LIST_COLS : (b + 1) * LIST_COLS]
+
+        ts_listed = held([P, B * N], F32, "ts_listed")
+        nc.vector.tensor_copy(ts_listed[:], ts_row[:].indirect(offsets[:]))
+        ts_col, ts_sq, ts_hi, ts_lo, wt_rows = [], [], [], [], []
+        for b in range(B):
+            turned = psum.tile([P, PACK, P], F32, name="ts_turned", tag="scores")
+            for t in range(PACK):
+                nc.tensor.transpose(turned[:, t, :], ts_listed[:, b * N + t : (b + 1) * N : PACK], identity[:])
+            ts_col.append(held([P, PACK], F32, "ts_col%d" % b))
+            ts_sq.append(held([P, PACK], F32, "ts_sq%d" % b))
+            ts_hi.append(held([P, PACK], F32, "ts_hi%d" % b))
+            ts_lo.append(held([P, PACK], F32, "ts_lo%d" % b))
+            nc.scalar.copy(ts_col[b][:], turned[:, :, 0])
+            nc.scalar.activation(ts_hi[b][:], turned[:, :, 0], ACT.Abs)
+            nc.gpsimd.tensor_tensor(ts_sq[b][:], ts_col[b][:], ts_col[b][:], ALU.mult)
+            nc.gpsimd.tensor_scalar(ts_lo[b][:], ts_hi[b][:], -1.0, 0.0, ALU.mult, ALU.add)
+            wt_rows.append(psum.tile([P, PACK, P], F32, name="wt_rows", tag="weights"))
+            for c in range(PACK):
+                nc.tensor.transpose(wt_rows[b][:, c, :], wt_cols[:, b, c : c + 1].to_broadcast([P, P]), identity[:])
+
+        w_listed = [held([P, PACK * N], BF16, "w_listed%d" % b) for b in range(B)]
+        w_by_slot = [held([P, D * PACK], BF16, "w_by_slot%d" % b) for b in range(B)]
+
+        def gather_plane(j, b):
+            plane = w_listed[b][:, j * N : (j + 1) * N]
+            nc.vector.tensor_copy(plane, table[j][:].indirect(group_offsets(b)))
+
+        def turn_plane(j, b):
+            words = w_listed[b][:, j * N : (j + 1) * N].bitcast(F32)
+            turned = psum.tile([P, 2, P], F32, name="w_turned", tag="result")
+            for u in range(2):
+                nc.tensor.transpose(turned[:, u, :], words[:, u : N // 2 : 2], identity[:])
+            dst = w_by_slot[b][:, j * P * PACK : (j + 1) * P * PACK].bitcast(F32)
+            nc.scalar.copy(dst.rearrange("p (m u) -> p m u", u=2), turned[:].rearrange("p u m -> p m u"))
+
+        def quantized(src, width, fmt, pool, name):
+            codes = pool.tile([P, width], U32, name=name + "_codes", align_bytes=64)
+            scales = pool.tile([P, width], U8, name=name + "_scales", align_bytes=64)
+            nc.vector.quantize_mx(out=codes[:].bitcast(fmt), scales=scales[:], in_=src)
+            return codes, scales
+
+        def quantized_by_place(src, name):
+            codes = held([P, N], U32, name + "_codes")
+            scales = held([P, N], U8, name + "_scales")
+            for t in range(PACK):
+                cols = slice(t * P, (t + 1) * P)
+                nc.vector.quantize_mx(
+                    out=codes[:, cols].bitcast(E4M3), scales=scales[:, cols], in_=src[:, t * N : (t + 1) * N]
+                )
+            return codes, scales
+
+        def weave_w(b, copy):
+            w_by_d = held([P, N * PACK], BF16, "w_by_d%d" % b)
+            copy(
+                w_by_d[:].rearrange("p (t c i j) -> p c j i t", t=PACK, i=2, j=PACK),
+                w_listed[b][:].rearrange("p (j c i t) -> p c j i t", j=PACK, i=2, t=PACK),
+            )
+            return w_by_d
+
+        def weave_x(b, copy):
+            x_by_d = held([P, R * PACK], BF16, "x_by_d%d" % b)
+            copy(
+                x_by_d[:].rearrange("p (c i j) -> p c j i", i=4, j=PACK),
+                x_raw[b][:].rearrange("p j (c i) -> p c j i", i=4),
+            )
+            return x_by_d
+
+        def scaled_targets(b, t):
+            turned = psum.tile([P, PACK, P], F32, name="y_turned", tag="targets")
+            for c in range(PACK):
+                nc.tensor.transpose(turned[:, c, :], y_raw[b][:, c, t:N:PACK], identity[:])
+            ty = ring.tile([P, R], F32, name="ty", bufs=PACK)
+            nc.scalar.activation(
+                ty[:].rearrange("p (m c) -> p m c", c=PACK),
+                turned[:].rearrange("p c m -> p m c"),
+                ACT.Copy,
+                scale=ts_col[b][:, t : t + 1],
+            )
+            return ty
+
+        def residual(b, t, w_q, x_q, ty):
+            scores = psum.tile([P, R], F32, name="scores", tag="scores")
+            cols = slice(t * P, (t + 1) * P)
+            nc.tensor.matmul_mx(
+                out=scores[:],
+                lhsT=w_q[0][:, cols].bitcast(E4M3),
+                lhsT_scale=w_q[1][:, cols],
+                rhs=x_q[0][:].bitcast(E4M3),
+                rhs_scale=x_q[1][:],
+                start=True,
+                stop=True,
+            )
+            diff = ring.tile([P, R], F32, name="diff")
+            nc.vector.scalar_tensor_tensor(diff[:], scores[:], ts_sq[b][:, t : t + 1], ty[:], ALU.mult, ALU.subtract)
+            return diff
+
+        def clip(b, t, diff, clipped):
+            nc.vector.tensor_scalar(
+                clipped[:, t, :], diff[:], ts_lo[b][:, t : t + 1], ts_hi[b][:, t : t + 1], ALU.max, ALU.min
+            )
+
+        def weigh(b, k, clipped):
+            h = ring.tile([P, P * PACK], BF16, name="h", align_bytes=64)
+            quads = P // 4
+            weights = wt_rows[b][:].rearrange("p i c -> p c i")[:, k * quads : (k + 1) * quads, :]
+            nc.vector.tensor_tensor(
+                h[:].rearrange("p (c i t) -> p c t i", i=4, t=PACK),
+                clipped[:, :, k * P : (k + 1) * P].rearrange("p t (c i) -> p c t i", i=4),
+                weights.unsqueeze(2).to_broadcast([P, quads, PACK, 4]),
+                ALU.mult,
+            )
+            return h
+
+        def finish(b, k, h, ws_q):
+            h_q = quantized(h[:], P, E5M2, ring, "h")
+            grad = psum.tile([P, D], F32, name="grad", tag="result")
+            nc.tensor.matmul_mx(
+                out=grad[:],
+                lhsT=h_q[0][:].bitcast(E5M2),
+                lhsT_scale=h_q[1][:],
+                rhs=ws_q[0][:].bitcast(E4M3),
+                rhs_scale=ws_q[1][:],
+                start=True,
+                stop=True,
+            )
+            result = ring.tile([P, D], F32, name="result", bufs=B * PACK)
+            copy = nc.vector.tensor_copy if (b, k) == (B - 1, R // P - 1) else nc.scalar.copy
+            copy(
+                result[:].rearrange("p (m j) -> p m j", j=PACK), grad[:].rearrange("p (j m) -> p m j", j=PACK)
+            )
+            nc.sync.dma_start(out[b, k * P : (k + 1) * P, :], result[:])
+
+        def residuals(b, w_q, x_q, targets):
+            clipped = held([P, PACK, R], F32, "clipped%d" % b)
+            diffs = []
+            for t in range(PACK):
+                diffs.append(residual(b, t, w_q, x_q, targets[t]))
+                if t >= 1:
+                    clip(b, t - 1, diffs[t - 1], clipped)
+            return clipped, diffs[PACK - 1]
+
+        def gradients(b, clipped, ws_q):
+            hs = []
+            for k in range(R // P):
+                hs.append(weigh(b, k, clipped))
+                if k >= 1:
+                    finish(b, k - 1, hs[k - 1], ws_q)
+            finish(b, R // P - 1, hs[-1], ws_q)
+
+        for j in range(PACK - 1):
+            for b in range(B):
+                gather_plane(j, b)
+                turn_plane(j, b)
+        gather_plane(PACK - 1, 0)
+        turn_plane(PACK - 1, 0)
+        gather_plane(PACK - 1, 1)
+        turn_plane(PACK - 1, 1)
+        for b in range(B):
+            load_group(b)
+        w_by_d0 = weave_w(0, nc.scalar.copy)
+        targets0 = [scaled_targets(0, t) for t in range(PACK)]
+        ws_q0 = quantized(w_by_slot[0][:], D, E4M3, keep, "ws_q0")
+        x_by_d0 = weave_x(0, nc.vector.tensor_copy)
+        x_q0 = quantized(x_by_d0[:], R, E4M3, keep, "x_q0")
+        w_q0 = quantized_by_place(w_by_d0, "w_q0")
+        clipped0, last0 = residuals(0, w_q0, x_q0, targets0)
+        ws_q1 = quantized(w_by_slot[1][:], D, E4M3, keep, "ws_q1")
+        clip(0, PACK - 1, last0, clipped0)
+        w_by_d1 = weave_w(1, nc.scalar.copy)
+        x_by_d1 = weave_x(1, nc.scalar.copy)
+        targets1 = [scaled_targets(1, t) for t in range(PACK)]
+        w_q1 = quantized(w_by_d1[:], N, E4M3, keep, "w_q1")
+        x_q1 = quantized(x_by_d1[:], R, E4M3, keep, "x_q1")
+        gradients(0, clipped0, ws_q0)
+        clipped1, last1 = residuals(1, w_q1, x_q1, targets1)
+        clip(1, PACK - 1, last1, clipped1)
+        gradients(1, clipped1, ws_q1)

@@ -19,39 +19,36 @@ ACT = mybir.ActivationFunctionType
 P = 128
 PACK = 4
 LIST_COLS = N // 16
+TILES = R // P
 
 
 def tile_attend_ghub_x_ts_kernel(tc, xT, wT, y, wt, ts, offs, out):
     nc = tc.nc
     with ExitStack() as ctx:
         keep = ctx.enter_context(tc.tile_pool(name="keep", bufs=1))
-        ring = ctx.enter_context(tc.tile_pool(name="ring", bufs=3))
-        stage = ctx.enter_context(tc.tile_pool(name="stage", bufs=PACK))
-        psum = ctx.enter_context(tc.psum_pool(name="psum", bufs=2))
+        ring = ctx.enter_context(tc.tile_pool(name="ring", bufs=TILES))
+        psum = ctx.enter_context(tc.psum_pool(name="psum", bufs=1))
 
-        def held(shape, dtype, name):
-            return keep.tile(shape, dtype, name=name, align_bytes=64)
+        def held(shape, dtype, name, tag=None):
+            return keep.tile(shape, dtype, name=name, tag=tag or name, align_bytes=64)
+
+        weight_bank = [psum.tile([P, R], F32, name="weight_bank%d" % b) for b in range(B)]
+        result_bank = [psum.tile([P, D], F32, name="result_bank%d" % i) for i in range(2)]
+        place_bank = [psum.tile([P, R], F32, name="place_bank%d" % t) for t in range(PACK)]
 
         offsets = keep.tile([P, B * LIST_COLS], U16, name="offsets")
         nc.sync.dma_start(offsets[:], offs)
-        ts_row = held([P, T], F32, "ts_row")
-        nc.sync.dma_start(ts_row[0:32, :], ts[0:32, :])
-        nc.gpsimd.memset(ts_row[32:64, :], 0.0)
-        nc.vector.memset(ts_row[64:P, :], 0.0)
-        wt_cols = held([P, B, PACK], F32, "wt_cols")
-        nc.scalar.dma_start(wt_cols[:], wt.rearrange("b (p c) o -> p b (c o)", c=PACK))
         w_planes = wT.rearrange("(p j) t -> p j t", j=PACK)
-        table = []
-        for j in range(PACK):
-            table.append(stage.tile([P, T], F32, name="table", tag="staged"))
+        table = [held([P, T], F32, "table%d" % j, "staged%d" % j) for j in range(PACK)]
+        nc.sync.dma_start(table[0][:], w_planes[:, 0, :])
+        wt_cols = held([P, B, PACK], F32, "wt_cols")
+        nc.sync.dma_start(wt_cols[:], wt.rearrange("b (p c) o -> p b (c o)", c=PACK))
+        ts_row = held([P, T], F32, "ts_row")
+        nc.gpsimd.memset(ts_row[:, : T // 2], 0.0)
+        nc.vector.memset(ts_row[:, T // 2 :], 0.0)
+        nc.sync.dma_start(ts_row[0:1, :], ts[0:1, :])
+        for j in range(1, PACK):
             nc.sync.dma_start(table[j][:], w_planes[:, j, :])
-        x_raw, y_raw = [], []
-
-        def load_group(b):
-            y_raw.append(stage.tile([P, PACK, N], F32, name="y_raw", tag="staged"))
-            nc.sync.dma_start(y_raw[b][:], y[b].rearrange("(p c) n -> p c n", c=PACK))
-            x_raw.append(stage.tile([P, PACK, R], F32, name="x_raw", tag="staged"))
-            nc.sync.dma_start(x_raw[b][:], xT[b].rearrange("(p j) r -> p j r", j=PACK))
 
         identity = held([P, P], F32, "identity")
         make_identity(nc, identity[:])
@@ -59,90 +56,94 @@ def tile_attend_ghub_x_ts_kernel(tc, xT, wT, y, wt, ts, offs, out):
         def group_offsets(b):
             return offsets[:, b * LIST_COLS : (b + 1) * LIST_COLS]
 
-        ts_listed = held([P, B * N], F32, "ts_listed")
-        nc.vector.tensor_copy(ts_listed[:], ts_row[:].indirect(offsets[:]))
-        ts_col, ts_sq, ts_hi, ts_lo, wt_rows = [], [], [], [], []
-        for b in range(B):
-            turned = psum.tile([P, PACK, P], F32, name="ts_turned", tag="scores")
-            for t in range(PACK):
-                nc.tensor.transpose(turned[:, t, :], ts_listed[:, b * N + t : (b + 1) * N : PACK], identity[:])
-            ts_col.append(held([P, PACK], F32, "ts_col%d" % b))
-            ts_sq.append(held([P, PACK], F32, "ts_sq%d" % b))
-            ts_hi.append(held([P, PACK], F32, "ts_hi%d" % b))
-            ts_lo.append(held([P, PACK], F32, "ts_lo%d" % b))
-            nc.scalar.copy(ts_col[b][:], turned[:, :, 0])
-            nc.scalar.activation(ts_hi[b][:], turned[:, :, 0], ACT.Abs)
-            nc.gpsimd.tensor_tensor(ts_sq[b][:], ts_col[b][:], ts_col[b][:], ALU.mult)
-            nc.gpsimd.tensor_scalar(ts_lo[b][:], ts_hi[b][:], -1.0, 0.0, ALU.mult, ALU.add)
-            wt_rows.append(psum.tile([P, PACK, P], F32, name="wt_rows", tag="weights"))
-            for c in range(PACK):
-                nc.tensor.transpose(wt_rows[b][:, c, :], wt_cols[:, b, c : c + 1].to_broadcast([P, P]), identity[:])
-
         w_listed = [held([P, PACK * N], BF16, "w_listed%d" % b) for b in range(B)]
-        w_by_slot = [held([P, D * PACK], BF16, "w_by_slot%d" % b) for b in range(B)]
+        w_by_slot = held([P, B * D * PACK], BF16, "w_by_slot")
 
         def gather_plane(j, b):
-            plane = w_listed[b][:, j * N : (j + 1) * N]
-            nc.vector.tensor_copy(plane, table[j][:].indirect(group_offsets(b)))
+            nc.vector.tensor_copy(w_listed[b][:, j * N : (j + 1) * N], table[j][:].indirect(group_offsets(b)))
 
-        def turn_plane(j, b):
-            words = w_listed[b][:, j * N : (j + 1) * N].bitcast(F32)
-            turned = psum.tile([P, 2, P], F32, name="w_turned", tag="result")
-            for u in range(2):
-                nc.tensor.transpose(turned[:, u, :], words[:, u : N // 2 : 2], identity[:])
-            dst = w_by_slot[b][:, j * P * PACK : (j + 1) * P * PACK].bitcast(F32)
-            nc.scalar.copy(dst.rearrange("p (m u) -> p m u", u=2), turned[:].rearrange("p u m -> p m u"))
+        table0_bf16 = held([P, T], BF16, "table0_bf16")
+        nc.scalar.activation(table0_bf16[:], table[0][:], ACT.Copy)
+        for b in range(B):
+            nc.scalar.activation(w_listed[b][:, 0:N], table0_bf16[:].indirect(group_offsets(b)), ACT.Copy)
 
-        def quantized(src, width, fmt, pool, name):
-            codes = pool.tile([P, width], U32, name=name + "_codes", align_bytes=64)
+        ts_listed = held([P, B * N], F32, "ts_listed")
+        nc.vector.tensor_copy(ts_listed[:], ts_row[:].indirect(offsets[:]))
+        ts_cols = held([P, 2, B, 8], F32, "ts_cols", "table0_bf16")
+        ts_made = held([P, 2, B, 8], F32, "ts_made")
+        ts_col = [ts_cols[:, 0, b, 0:PACK] for b in range(B)]
+        ts_hi = [ts_cols[:, 1, b, 0:PACK] for b in range(B)]
+        ts_sq = [ts_made[:, 0, b, 0:PACK] for b in range(B)]
+        ts_lo = [ts_made[:, 1, b, 0:PACK] for b in range(B)]
+        for b in range(B):
+            turned = place_bank[b][:].rearrange("p (t m) -> p t m", t=PACK)
+            for t in range(PACK):
+                nc.tensor.transpose(turned[:, t, :], ts_listed[:, b * N + t : (b + 1) * N : PACK], identity[:])
+            nc.scalar.copy(ts_col[b], turned[:, :, 0])
+            nc.scalar.activation(ts_hi[b], turned[:, :, 0], ACT.Abs)
+            nc.gpsimd.tensor_tensor(ts_sq[b], ts_col[b], ts_col[b], ALU.mult)
+            nc.gpsimd.tensor_scalar(ts_lo[b], ts_hi[b], -1.0, 0.0, ALU.mult, ALU.add)
+            for c in range(PACK):
+                nc.tensor.transpose(
+                    weight_bank[b][:, c * P : (c + 1) * P], wt_cols[:, b, c : c + 1].to_broadcast([P, P]), identity[:]
+                )
+
+        def turn_plane(j, groups, bank):
+            turned = bank[:].rearrange("p (b u m) -> p b u m", b=B, u=2)
+            for b in range(groups.start, groups.stop):
+                words = w_listed[b][:, j * N : (j + 1) * N].bitcast(F32)
+                for u in range(2):
+                    nc.tensor.transpose(turned[:, b, u, :], words[:, u : N // 2 : 2], identity[:])
+            dst = w_by_slot[:].bitcast(F32).rearrange("p (b j m u) -> p b j m u", b=B, j=PACK, u=2)
+            nc.scalar.copy(dst[:, groups, j, :, :], turned[:, groups, :, :].rearrange("p b u m -> p b m u"))
+
+        def quantized(src, width, fmt, pool, name, tag=None):
+            codes = pool.tile([P, width], U32, name=name + "_codes", tag=tag or name + "_codes", align_bytes=64)
             scales = pool.tile([P, width], U8, name=name + "_scales", align_bytes=64)
             nc.vector.quantize_mx(out=codes[:].bitcast(fmt), scales=scales[:], in_=src)
             return codes, scales
 
-        def quantized_by_place(src, name):
-            codes = held([P, N], U32, name + "_codes")
-            scales = held([P, N], U8, name + "_scales")
-            for t in range(PACK):
-                cols = slice(t * P, (t + 1) * P)
-                nc.vector.quantize_mx(
-                    out=codes[:, cols].bitcast(E4M3), scales=scales[:, cols], in_=src[:, t * N : (t + 1) * N]
-                )
-            return codes, scales
+        w_by_d = [held([P, N * PACK], BF16, "w_by_d%d" % b) for b in range(B)]
 
-        def weave_w(b, copy):
-            w_by_d = held([P, N * PACK], BF16, "w_by_d%d" % b)
+        def weave_w(b, planes, copy):
             copy(
-                w_by_d[:].rearrange("p (t c i j) -> p c j i t", t=PACK, i=2, j=PACK),
-                w_listed[b][:].rearrange("p (j c i t) -> p c j i t", j=PACK, i=2, t=PACK),
+                w_by_d[b][:].rearrange("p (t c i j) -> p c j i t", t=PACK, i=2, j=PACK)[:, :, planes],
+                w_listed[b][:].rearrange("p (j c i t) -> p c j i t", j=PACK, i=2, t=PACK)[:, :, planes],
             )
-            return w_by_d
 
-        def weave_x(b, copy):
-            x_by_d = held([P, R * PACK], BF16, "x_by_d%d" % b)
+        def load_y(b, tag):
+            y_raw = held([P, PACK, N], F32, "y_raw%d" % b, tag)
+            nc.sync.dma_start(y_raw[:], y[b].rearrange("(p c) n -> p c n", c=PACK))
+            return y_raw
+
+        def load_x(b, tag):
+            x_raw = held([P, PACK, R], F32, "x_raw%d" % b, tag)
+            nc.sync.dma_start(x_raw[:], xT[b].rearrange("(p j) r -> p j r", j=PACK))
+            return x_raw
+
+        def weave_x(x_by_d, x_raw, quads, copy):
             copy(
-                x_by_d[:].rearrange("p (c i j) -> p c j i", i=4, j=PACK),
-                x_raw[b][:].rearrange("p j (c i) -> p c j i", i=4),
+                x_by_d[:].rearrange("p (c i j) -> p c j i", i=4, j=PACK)[:, quads],
+                x_raw[:].rearrange("p j (c i) -> p c j i", i=4)[:, quads],
             )
-            return x_by_d
 
-        def scaled_targets(b, t):
-            turned = psum.tile([P, PACK, P], F32, name="y_turned", tag="targets")
+        def scaled_targets(b, t, y_raw, bank):
+            turned = bank[:].rearrange("p (c m) -> p c m", c=PACK)
             for c in range(PACK):
-                nc.tensor.transpose(turned[:, c, :], y_raw[b][:, c, t:N:PACK], identity[:])
-            ty = ring.tile([P, R], F32, name="ty", bufs=PACK)
+                nc.tensor.transpose(turned[:, c, :], y_raw[:, c, t:N:PACK], identity[:])
+            ty = held([P, R], F32, "ty%d_%d" % (b, t), "ty%d" % t)
             nc.scalar.activation(
                 ty[:].rearrange("p (m c) -> p m c", c=PACK),
-                turned[:].rearrange("p c m -> p m c"),
+                turned.rearrange("p c m -> p m c"),
                 ACT.Copy,
                 scale=ts_col[b][:, t : t + 1],
             )
             return ty
 
-        def residual(b, t, w_q, x_q, ty):
-            scores = psum.tile([P, R], F32, name="scores", tag="scores")
+        def score(t, w_q, x_q, bank):
             cols = slice(t * P, (t + 1) * P)
             nc.tensor.matmul_mx(
-                out=scores[:],
+                out=bank[:],
                 lhsT=w_q[0][:, cols].bitcast(E4M3),
                 lhsT_scale=w_q[1][:, cols],
                 rhs=x_q[0][:].bitcast(E4M3),
@@ -150,8 +151,10 @@ def tile_attend_ghub_x_ts_kernel(tc, xT, wT, y, wt, ts, offs, out):
                 start=True,
                 stop=True,
             )
+
+        def residual(b, t, bank, ty):
             diff = ring.tile([P, R], F32, name="diff")
-            nc.vector.scalar_tensor_tensor(diff[:], scores[:], ts_sq[b][:, t : t + 1], ty[:], ALU.mult, ALU.subtract)
+            nc.vector.scalar_tensor_tensor(diff[:], bank[:], ts_sq[b][:, t : t + 1], ty[:], ALU.mult, ALU.subtract)
             return diff
 
         def clip(b, t, diff, clipped):
@@ -162,7 +165,7 @@ def tile_attend_ghub_x_ts_kernel(tc, xT, wT, y, wt, ts, offs, out):
         def weigh(b, k, clipped):
             h = ring.tile([P, P * PACK], BF16, name="h", align_bytes=64)
             quads = P // 4
-            weights = wt_rows[b][:].rearrange("p i c -> p c i")[:, k * quads : (k + 1) * quads, :]
+            weights = weight_bank[b][:].rearrange("p (i c) -> p c i", i=4)[:, k * quads : (k + 1) * quads, :]
             nc.vector.tensor_tensor(
                 h[:].rearrange("p (c i t) -> p c t i", i=4, t=PACK),
                 clipped[:, :, k * P : (k + 1) * P].rearrange("p t (c i) -> p c t i", i=4),
@@ -171,67 +174,83 @@ def tile_attend_ghub_x_ts_kernel(tc, xT, wT, y, wt, ts, offs, out):
             )
             return h
 
-        def finish(b, k, h, ws_q):
+        def finish(b, k, h, ws_q, grad):
             h_q = quantized(h[:], P, E5M2, ring, "h")
-            grad = psum.tile([P, D], F32, name="grad", tag="result")
+            cols = slice(b * D, (b + 1) * D)
             nc.tensor.matmul_mx(
                 out=grad[:],
                 lhsT=h_q[0][:].bitcast(E5M2),
                 lhsT_scale=h_q[1][:],
-                rhs=ws_q[0][:].bitcast(E4M3),
-                rhs_scale=ws_q[1][:],
+                rhs=ws_q[0][:, cols].bitcast(E4M3),
+                rhs_scale=ws_q[1][:, cols],
                 start=True,
                 stop=True,
             )
-            result = ring.tile([P, D], F32, name="result", bufs=B * PACK)
-            copy = nc.vector.tensor_copy if (b, k) == (B - 1, R // P - 1) else nc.scalar.copy
-            copy(
-                result[:].rearrange("p (m j) -> p m j", j=PACK), grad[:].rearrange("p (j m) -> p m j", j=PACK)
-            )
-            nc.sync.dma_start(out[b, k * P : (k + 1) * P, :], result[:])
+            result = held([P, D], F32, "result%d_%d" % (b, k))
+            last = (b, k) == (B - 1, TILES - 1)
+            copy = nc.vector.tensor_copy if last else nc.scalar.copy
+            pieces = 2 if last else 1
+            for i in range(pieces):
+                d_cols = slice(i * D // pieces, (i + 1) * D // pieces)
+                m_cols = slice(i * P // pieces, (i + 1) * P // pieces)
+                copy(
+                    result[:, d_cols].rearrange("p (m j) -> p m j", j=PACK),
+                    grad[:].rearrange("p (j m) -> p m j", j=PACK)[:, m_cols, :],
+                )
+                nc.sync.dma_start(out[b, k * P : (k + 1) * P, d_cols], result[:, d_cols])
+
+        def gradients(b, clipped, ws_q, banks):
+            hs = []
+            for k in range(TILES):
+                hs.append(weigh(b, k, clipped))
+                if k >= 1:
+                    finish(b, k - 1, hs[k - 1], ws_q, banks[k - 1])
+            finish(b, TILES - 1, hs[-1], ws_q, banks[-1])
 
         def residuals(b, w_q, x_q, targets):
             clipped = held([P, PACK, R], F32, "clipped%d" % b)
             diffs = []
             for t in range(PACK):
-                diffs.append(residual(b, t, w_q, x_q, targets[t]))
+                score(t, w_q, x_q, place_bank[t])
+                diffs.append(residual(b, t, place_bank[t], targets[t]))
                 if t >= 1:
                     clip(b, t - 1, diffs[t - 1], clipped)
             return clipped, diffs[PACK - 1]
 
-        def gradients(b, clipped, ws_q):
-            hs = []
-            for k in range(R // P):
-                hs.append(weigh(b, k, clipped))
-                if k >= 1:
-                    finish(b, k - 1, hs[k - 1], ws_q)
-            finish(b, R // P - 1, hs[-1], ws_q)
-
-        for j in range(PACK - 1):
-            for b in range(B):
-                gather_plane(j, b)
-                turn_plane(j, b)
-        gather_plane(PACK - 1, 0)
-        turn_plane(PACK - 1, 0)
-        gather_plane(PACK - 1, 1)
-        turn_plane(PACK - 1, 1)
+        last = PACK - 1
+        both = slice(0, B)
+        turn_plane(0, both, result_bank[0])
         for b in range(B):
-            load_group(b)
-        w_by_d0 = weave_w(0, nc.scalar.copy)
-        targets0 = [scaled_targets(0, t) for t in range(PACK)]
-        ws_q0 = quantized(w_by_slot[0][:], D, E4M3, keep, "ws_q0")
-        x_by_d0 = weave_x(0, nc.vector.tensor_copy)
-        x_q0 = quantized(x_by_d0[:], R, E4M3, keep, "x_q0")
-        w_q0 = quantized_by_place(w_by_d0, "w_q0")
-        clipped0, last0 = residuals(0, w_q0, x_q0, targets0)
-        ws_q1 = quantized(w_by_slot[1][:], D, E4M3, keep, "ws_q1")
-        clip(0, PACK - 1, last0, clipped0)
-        w_by_d1 = weave_w(1, nc.scalar.copy)
-        x_by_d1 = weave_x(1, nc.scalar.copy)
-        targets1 = [scaled_targets(1, t) for t in range(PACK)]
-        w_q1 = quantized(w_by_d1[:], N, E4M3, keep, "w_q1")
-        x_q1 = quantized(x_by_d1[:], R, E4M3, keep, "x_q1")
-        gradients(0, clipped0, ws_q0)
-        clipped1, last1 = residuals(1, w_q1, x_q1, targets1)
-        clip(1, PACK - 1, last1, clipped1)
-        gradients(1, clipped1, ws_q1)
+            gather_plane(1, b)
+        turn_plane(1, both, result_bank[1])
+        for b in range(B):
+            weave_w(b, slice(0, 2), nc.scalar.copy)
+        for b in range(B):
+            gather_plane(2, b)
+        turn_plane(2, both, place_bank[2])
+        for b in range(B):
+            gather_plane(last, b)
+        turn_plane(last, both, result_bank[0])
+        weave_w(0, slice(2, PACK), nc.vector.tensor_copy)
+        y_raw0 = load_y(0, "staged0")
+        x_raw0 = load_x(0, "staged1")
+        x_raw1 = load_x(1, "staged2")
+        y_raw1 = load_y(1, "staged3")
+        w_q0 = quantized(w_by_d[0][:], N, E4M3, keep, "w_q")
+        x_by_d0 = held([P, R * PACK], BF16, "x_by_d0")
+        weave_x(x_by_d0, x_raw0, slice(0, R // 4), nc.vector.tensor_copy)
+        targets0 = [scaled_targets(0, t, y_raw0, place_bank[t]) for t in range(PACK)]
+        x_q0 = quantized(x_by_d0[:], R, E4M3, keep, "x_q")
+        ws_q = quantized(w_by_slot[:], B * D, E4M3, keep, "ws_q", "x_by_d0")
+        weave_w(1, slice(2, PACK), nc.scalar.copy)
+        clipped0, diff0 = residuals(0, w_q0, x_q0, targets0)
+        w_q1 = quantized(w_by_d[1][:], N, E4M3, keep, "w_q")
+        clip(0, last, diff0, clipped0)
+        x_by_d1 = held([P, R * PACK], BF16, "x_by_d1", "staged0")
+        weave_x(x_by_d1, x_raw1, slice(0, R // 4), nc.scalar.copy)
+        targets1 = [scaled_targets(1, t, y_raw1, place_bank[t]) for t in range(PACK)]
+        x_q1 = quantized(x_by_d1[:], R, E4M3, keep, "x_q")
+        gradients(0, clipped0, ws_q, result_bank + result_bank)
+        clipped1, diff1 = residuals(1, w_q1, x_q1, targets1)
+        clip(1, last, diff1, clipped1)
+        gradients(1, clipped1, ws_q, place_bank)

@@ -158,8 +158,9 @@ def tile_attend_ghub_x_ts_kernel(tc, xT, wT, y, wt, ts, offs, out):
             return diff
 
         def clip(b, t, diff, clipped):
-            nc.vector.tensor_scalar(
-                clipped[:, t, :], diff[:], ts_lo[b][:, t : t + 1], ts_hi[b][:, t : t + 1], ALU.max, ALU.min
+            engine = nc.gpsimd if t < 2 else nc.vector
+            engine.tensor_scalar(
+                clipped[:, t, :], diff[:], ts_hi[b][:, t : t + 1], ts_lo[b][:, t : t + 1], ALU.min, ALU.max
             )
 
         def weigh(b, k, clipped):

@@ -18,15 +18,18 @@ ACT = mybir.ActivationFunctionType
 
 P = 128
 PACK = 4
+LAST = PACK - 1
 LIST_COLS = N // 16
-TILES = R // P
+ROW_TILES = R // P
+QUAD = 4
+GPSIMD_PLACES = 2
 
 
 def tile_attend_ghub_x_ts_kernel(tc, xT, wT, y, wt, ts, offs, out):
     nc = tc.nc
     with ExitStack() as ctx:
         keep = ctx.enter_context(tc.tile_pool(name="keep", bufs=1))
-        ring = ctx.enter_context(tc.tile_pool(name="ring", bufs=TILES))
+        ring = ctx.enter_context(tc.tile_pool(name="ring", bufs=ROW_TILES))
         psum = ctx.enter_context(tc.psum_pool(name="psum", bufs=1))
 
         def held(shape, dtype, name, tag=None):
@@ -37,30 +40,55 @@ def tile_attend_ghub_x_ts_kernel(tc, xT, wT, y, wt, ts, offs, out):
         place_bank = [psum.tile([P, R], F32, name="place_bank%d" % t) for t in range(PACK)]
 
         offsets = keep.tile([P, B * LIST_COLS], U16, name="offsets")
-        nc.sync.dma_start(offsets[:], offs)
         w_planes = wT.rearrange("(p j) t -> p j t", j=PACK)
         table = [held([P, T], F32, "table%d" % j, "staged%d" % j) for j in range(PACK)]
         nc.sync.dma_start(table[0][:], w_planes[:, 0, :])
-        wt_cols = held([P, B, PACK], F32, "wt_cols")
-        nc.sync.dma_start(wt_cols[:], wt.rearrange("b (p c) o -> p b (c o)", c=PACK))
+        nc.sync.dma_start(offsets[:], offs)
         ts_row = held([P, T], F32, "ts_row")
         nc.gpsimd.memset(ts_row[:, : T // 2], 0.0)
         nc.vector.memset(ts_row[:, T // 2 :], 0.0)
         nc.sync.dma_start(ts_row[0:1, :], ts[0:1, :])
+        wt_rows = held([P, P], F32, "wt_rows")
+        nc.gpsimd.memset(wt_rows[:], 0.0)
+        nc.sync.dma_start(wt_rows[0 : B * ROW_TILES, :], wt.rearrange("b (k m) o -> (b k) (m o)", m=P))
         for j in range(1, PACK):
             nc.sync.dma_start(table[j][:], w_planes[:, j, :])
 
         identity = held([P, P], F32, "identity")
         make_identity(nc, identity[:])
 
+        nc.tensor.transpose(weight_bank[0][:, 0:P], wt_rows[:], identity[:])
+        wt_cols = held([P, B * ROW_TILES], F32, "wt_cols")
+        nc.scalar.copy(wt_cols[:], weight_bank[0][:, 0 : B * ROW_TILES])
+        for b in range(B):
+            for k in range(ROW_TILES):
+                column = wt_cols[:, b * ROW_TILES + k : b * ROW_TILES + k + 1]
+                nc.tensor.transpose(weight_bank[b][:, k * P : (k + 1) * P], column.to_broadcast([P, P]), identity[:])
+
         def group_offsets(b):
             return offsets[:, b * LIST_COLS : (b + 1) * LIST_COLS]
 
         w_listed = [held([P, PACK * N], BF16, "w_listed%d" % b) for b in range(B)]
         w_by_slot = held([P, B * D * PACK], BF16, "w_by_slot")
+        w_by_d = [held([P, N * PACK], BF16, "w_by_d%d" % b) for b in range(B)]
 
         def gather_plane(j, b):
             nc.vector.tensor_copy(w_listed[b][:, j * N : (j + 1) * N], table[j][:].indirect(group_offsets(b)))
+
+        def weave_w(b, planes, copy):
+            copy(
+                w_by_d[b][:].rearrange("p (t c i j) -> p c j i t", t=PACK, i=2, j=PACK)[:, :, planes],
+                w_listed[b][:].rearrange("p (j c i t) -> p c j i t", j=PACK, i=2, t=PACK)[:, :, planes],
+            )
+
+        def turn_plane(j, bank):
+            turned = bank[:].rearrange("p (b u m) -> p b u m", b=B, u=2)
+            for b in range(B):
+                words = w_listed[b][:, j * N : (j + 1) * N].bitcast(F32)
+                for u in range(2):
+                    nc.tensor.transpose(turned[:, b, u, :], words[:, u : N // 2 : 2], identity[:])
+            by_slot = w_by_slot[:].bitcast(F32).rearrange("p (b j m u) -> p b j m u", b=B, j=PACK, u=2)
+            nc.scalar.copy(by_slot[:, :, j, :, :], turned.rearrange("p b u m -> p b m u"))
 
         table0_bf16 = held([P, T], BF16, "table0_bf16")
         nc.scalar.activation(table0_bf16[:], table[0][:], ACT.Copy)
@@ -69,46 +97,47 @@ def tile_attend_ghub_x_ts_kernel(tc, xT, wT, y, wt, ts, offs, out):
 
         ts_listed = held([P, B * N], F32, "ts_listed")
         nc.vector.tensor_copy(ts_listed[:], ts_row[:].indirect(offsets[:]))
-        ts_cols = held([P, 2, B, 8], F32, "ts_cols", "table0_bf16")
-        ts_made = held([P, 2, B, 8], F32, "ts_made")
-        ts_col = [ts_cols[:, 0, b, 0:PACK] for b in range(B)]
-        ts_hi = [ts_cols[:, 1, b, 0:PACK] for b in range(B)]
-        ts_sq = [ts_made[:, 0, b, 0:PACK] for b in range(B)]
-        ts_lo = [ts_made[:, 1, b, 0:PACK] for b in range(B)]
+        for b in range(B):
+            gather_plane(1, b)
+            weave_w(b, slice(0, 2), nc.scalar.copy)
+
+        ts_read = held([P, 2, B, PACK], F32, "ts_read", "table0_bf16")
+        ts_made = held([P, 2, B, PACK], F32, "ts_made")
+        ts_col = [ts_read[:, 0, b, :] for b in range(B)]
+        ts_abs = [ts_read[:, 1, b, :] for b in range(B)]
+        ts_square = [ts_made[:, 0, b, :] for b in range(B)]
+        ts_minus_abs = [ts_made[:, 1, b, :] for b in range(B)]
         for b in range(B):
             turned = place_bank[b][:].rearrange("p (t m) -> p t m", t=PACK)
             for t in range(PACK):
                 nc.tensor.transpose(turned[:, t, :], ts_listed[:, b * N + t : (b + 1) * N : PACK], identity[:])
             nc.scalar.copy(ts_col[b], turned[:, :, 0])
-            nc.scalar.activation(ts_hi[b], turned[:, :, 0], ACT.Abs)
-            nc.gpsimd.tensor_tensor(ts_sq[b], ts_col[b], ts_col[b], ALU.mult)
-            nc.gpsimd.tensor_scalar(ts_lo[b], ts_hi[b], -1.0, 0.0, ALU.mult, ALU.add)
-            for c in range(PACK):
-                nc.tensor.transpose(
-                    weight_bank[b][:, c * P : (c + 1) * P], wt_cols[:, b, c : c + 1].to_broadcast([P, P]), identity[:]
-                )
+            nc.scalar.activation(ts_abs[b], turned[:, :, 0], ACT.Abs)
+            nc.gpsimd.tensor_tensor(ts_square[b], ts_col[b], ts_col[b], ALU.mult)
+            nc.gpsimd.tensor_scalar(ts_minus_abs[b], ts_abs[b], -1.0, 0.0, ALU.mult, ALU.add)
 
-        def turn_plane(j, groups, bank):
-            turned = bank[:].rearrange("p (b u m) -> p b u m", b=B, u=2)
-            for b in range(groups.start, groups.stop):
-                words = w_listed[b][:, j * N : (j + 1) * N].bitcast(F32)
-                for u in range(2):
-                    nc.tensor.transpose(turned[:, b, u, :], words[:, u : N // 2 : 2], identity[:])
-            dst = w_by_slot[:].bitcast(F32).rearrange("p (b j m u) -> p b j m u", b=B, j=PACK, u=2)
-            nc.scalar.copy(dst[:, groups, j, :, :], turned[:, groups, :, :].rearrange("p b u m -> p b m u"))
-
-        def quantized(src, width, fmt, pool, name, tag=None):
+        def packed(width, pool, name, tag=None):
             codes = pool.tile([P, width], U32, name=name + "_codes", tag=tag or name + "_codes", align_bytes=64)
             scales = pool.tile([P, width], U8, name=name + "_scales", align_bytes=64)
-            nc.vector.quantize_mx(out=codes[:].bitcast(fmt), scales=scales[:], in_=src)
             return codes, scales
 
-        w_by_d = [held([P, N * PACK], BF16, "w_by_d%d" % b) for b in range(B)]
+        def quantize(operand, columns, values, fmt):
+            nc.vector.quantize_mx(out=operand[0][:, columns].bitcast(fmt), scales=operand[1][:, columns], in_=values)
 
-        def weave_w(b, planes, copy):
-            copy(
-                w_by_d[b][:].rearrange("p (t c i j) -> p c j i t", t=PACK, i=2, j=PACK)[:, :, planes],
-                w_listed[b][:].rearrange("p (j c i t) -> p c j i t", j=PACK, i=2, t=PACK)[:, :, planes],
+        def quantized(values, width, fmt, pool, name, tag=None):
+            operand = packed(width, pool, name, tag)
+            quantize(operand, slice(0, width), values, fmt)
+            return operand
+
+        def multiply(bank, stationary, m_cols, fmt, moving, n_cols):
+            nc.tensor.matmul_mx(
+                out=bank[:],
+                lhsT=stationary[0][:, m_cols].bitcast(fmt),
+                lhsT_scale=stationary[1][:, m_cols],
+                rhs=moving[0][:, n_cols].bitcast(E4M3),
+                rhs_scale=moving[1][:, n_cols],
+                start=True,
+                stop=True,
             )
 
         def load_y(b, tag):
@@ -121,137 +150,126 @@ def tile_attend_ghub_x_ts_kernel(tc, xT, wT, y, wt, ts, offs, out):
             nc.sync.dma_start(x_raw[:], xT[b].rearrange("(p j) r -> p j r", j=PACK))
             return x_raw
 
-        def weave_x(x_by_d, x_raw, quads, copy):
+        def weave_x(x_by_d, x_raw, rows, copy):
+            quads = slice(rows.start // QUAD, rows.stop // QUAD)
             copy(
-                x_by_d[:].rearrange("p (c i j) -> p c j i", i=4, j=PACK)[:, quads],
-                x_raw[:].rearrange("p j (c i) -> p c j i", i=4)[:, quads],
+                x_by_d[:].rearrange("p (c i j) -> p c j i", i=QUAD, j=PACK)[:, quads],
+                x_raw[:].rearrange("p j (c i) -> p c j i", i=QUAD)[:, quads],
             )
 
-        def scaled_targets(b, t, y_raw, bank):
-            turned = bank[:].rearrange("p (c m) -> p c m", c=PACK)
+        def scaled_targets(b, t, y_raw):
+            turned = place_bank[t][:].rearrange("p (c m) -> p c m", c=PACK)
             for c in range(PACK):
                 nc.tensor.transpose(turned[:, c, :], y_raw[:, c, t:N:PACK], identity[:])
-            ty = held([P, R], F32, "ty%d_%d" % (b, t), "ty%d" % t)
+            target = held([P, R], F32, "target%d_%d" % (b, t), "target%d" % t)
             nc.scalar.activation(
-                ty[:].rearrange("p (m c) -> p m c", c=PACK),
+                target[:].rearrange("p (m c) -> p m c", c=PACK),
                 turned.rearrange("p c m -> p m c"),
                 ACT.Copy,
                 scale=ts_col[b][:, t : t + 1],
             )
-            return ty
+            return target
 
-        def score(t, w_q, x_q, bank):
-            cols = slice(t * P, (t + 1) * P)
-            nc.tensor.matmul_mx(
-                out=bank[:],
-                lhsT=w_q[0][:, cols].bitcast(E4M3),
-                lhsT_scale=w_q[1][:, cols],
-                rhs=x_q[0][:].bitcast(E4M3),
-                rhs_scale=x_q[1][:],
-                start=True,
-                stop=True,
-            )
-
-        def residual(b, t, bank, ty):
-            diff = ring.tile([P, R], F32, name="diff")
-            nc.vector.scalar_tensor_tensor(diff[:], bank[:], ts_sq[b][:, t : t + 1], ty[:], ALU.mult, ALU.subtract)
-            return diff
-
-        def clip(b, t, diff, clipped):
-            engine = nc.gpsimd if t < 2 else nc.vector
+        def clip(b, t, residual, clipped, rows):
+            engine = nc.gpsimd if t < GPSIMD_PLACES else nc.vector
             engine.tensor_scalar(
-                clipped[:, t, :], diff[:], ts_hi[b][:, t : t + 1], ts_lo[b][:, t : t + 1], ALU.min, ALU.max
+                clipped[:, t, rows],
+                residual[:, rows],
+                ts_abs[b][:, t : t + 1],
+                ts_minus_abs[b][:, t : t + 1],
+                ALU.min,
+                ALU.max,
             )
 
-        def weigh(b, k, clipped):
-            h = ring.tile([P, P * PACK], BF16, name="h", align_bytes=64)
-            quads = P // 4
-            weights = weight_bank[b][:].rearrange("p (i c) -> p c i", i=4)[:, k * quads : (k + 1) * quads, :]
+        def residuals(b, w_q, x_q, targets):
+            clipped = held([P, PACK, R], F32, "clipped%d" % b)
+            residual = []
+            for t in range(PACK):
+                multiply(place_bank[t], w_q, slice(t * P, (t + 1) * P), E4M3, x_q, all_rows)
+                residual.append(ring.tile([P, R], F32, name="residual"))
+                nc.vector.scalar_tensor_tensor(
+                    residual[t][:], place_bank[t][:], ts_square[b][:, t : t + 1], targets[t][:], ALU.mult, ALU.subtract
+                )
+                if t >= 1:
+                    clip(b, t - 1, residual[t - 1], clipped, all_rows)
+            return clipped, residual[LAST]
+
+        def weigh(b, rows, clipped):
+            count = rows.stop - rows.start
+            h = ring.tile([P, count * PACK], BF16, name="h", align_bytes=64)
+            weights = weight_bank[b][:, rows].rearrange("p (c i) -> p c i", i=QUAD)
             nc.vector.tensor_tensor(
-                h[:].rearrange("p (c i t) -> p c t i", i=4, t=PACK),
-                clipped[:, :, k * P : (k + 1) * P].rearrange("p t (c i) -> p c t i", i=4),
-                weights.unsqueeze(2).to_broadcast([P, quads, PACK, 4]),
+                h[:].rearrange("p (c i t) -> p c t i", i=QUAD, t=PACK),
+                clipped[:, :, rows].rearrange("p t (c i) -> p c t i", i=QUAD),
+                weights.unsqueeze(2).to_broadcast([P, count // QUAD, PACK, QUAD]),
                 ALU.mult,
             )
             return h
 
-        def finish(b, k, h, ws_q, grad):
-            h_q = quantized(h[:], P, E5M2, ring, "h")
-            cols = slice(b * D, (b + 1) * D)
-            nc.tensor.matmul_mx(
-                out=grad[:],
-                lhsT=h_q[0][:].bitcast(E5M2),
-                lhsT_scale=h_q[1][:],
-                rhs=ws_q[0][:, cols].bitcast(E4M3),
-                rhs_scale=ws_q[1][:, cols],
-                start=True,
-                stop=True,
-            )
-            result = held([P, D], F32, "result%d_%d" % (b, k))
-            last = (b, k) == (B - 1, TILES - 1)
-            copy = nc.vector.tensor_copy if last else nc.scalar.copy
-            pieces = 2 if last else 1
-            for i in range(pieces):
-                d_cols = slice(i * D // pieces, (i + 1) * D // pieces)
-                m_cols = slice(i * P // pieces, (i + 1) * P // pieces)
-                copy(
-                    result[:, d_cols].rearrange("p (m j) -> p m j", j=PACK),
-                    grad[:].rearrange("p (j m) -> p m j", j=PACK)[:, m_cols, :],
-                )
-                nc.sync.dma_start(out[b, k * P : (k + 1) * P, d_cols], result[:, d_cols])
+        def finish(b, rows, h, w_slot_q, banks):
+            h_q = quantized(h[:], rows.stop - rows.start, E5M2, ring, "h")
+            for k in range(rows.start // P, rows.stop // P):
+                tile_rows = slice(k * P - rows.start, (k + 1) * P - rows.start)
+                multiply(banks[k], h_q, tile_rows, E5M2, w_slot_q, slice(b * D, (b + 1) * D))
+                result = held([P, D], F32, "result%d_%d" % (b, k))
+                final = (b, k) == (B - 1, ROW_TILES - 1)
+                copy = nc.vector.tensor_copy if final else nc.scalar.copy
+                pieces = 2 if final else 1
+                for i in range(pieces):
+                    d_cols = slice(i * D // pieces, (i + 1) * D // pieces)
+                    m_cols = slice(i * P // pieces, (i + 1) * P // pieces)
+                    copy(
+                        result[:, d_cols].rearrange("p (m j) -> p m j", j=PACK),
+                        banks[k][:].rearrange("p (j m) -> p m j", j=PACK)[:, m_cols, :],
+                    )
+                    nc.sync.dma_start(out[b, k * P : (k + 1) * P, d_cols], result[:, d_cols])
 
-        def gradients(b, clipped, ws_q, banks):
+        def gradients(b, clipped, w_slot_q, banks, span):
+            spans = [slice(r, r + span) for r in range(0, R, span)]
             hs = []
-            for k in range(TILES):
-                hs.append(weigh(b, k, clipped))
-                if k >= 1:
-                    finish(b, k - 1, hs[k - 1], ws_q, banks[k - 1])
-            finish(b, TILES - 1, hs[-1], ws_q, banks[-1])
+            for i, rows in enumerate(spans):
+                hs.append(weigh(b, rows, clipped))
+                if i >= 1:
+                    finish(b, spans[i - 1], hs[i - 1], w_slot_q, banks)
+            finish(b, spans[-1], hs[-1], w_slot_q, banks)
 
-        def residuals(b, w_q, x_q, targets):
-            clipped = held([P, PACK, R], F32, "clipped%d" % b)
-            diffs = []
-            for t in range(PACK):
-                score(t, w_q, x_q, place_bank[t])
-                diffs.append(residual(b, t, place_bank[t], targets[t]))
-                if t >= 1:
-                    clip(b, t - 1, diffs[t - 1], clipped)
-            return clipped, diffs[PACK - 1]
+        all_rows = slice(0, R)
+        halves = [slice(0, R // 2), slice(R // 2, R)]
 
-        last = PACK - 1
-        both = slice(0, B)
-        turn_plane(0, both, result_bank[0])
-        for b in range(B):
-            gather_plane(1, b)
-        turn_plane(1, both, result_bank[1])
-        for b in range(B):
-            weave_w(b, slice(0, 2), nc.scalar.copy)
-        for b in range(B):
-            gather_plane(2, b)
-        turn_plane(2, both, place_bank[2])
-        for b in range(B):
-            gather_plane(last, b)
-        turn_plane(last, both, result_bank[0])
+        turn_plane(0, result_bank[0])
+        turn_plane(1, result_bank[1])
+        for j in range(2, PACK):
+            for b in range(B):
+                gather_plane(j, b)
+            turn_plane(j, place_bank[j])
         weave_w(0, slice(2, PACK), nc.vector.tensor_copy)
+
         y_raw0 = load_y(0, "staged0")
         x_raw0 = load_x(0, "staged1")
         x_raw1 = load_x(1, "staged2")
         y_raw1 = load_y(1, "staged3")
+
         w_q0 = quantized(w_by_d[0][:], N, E4M3, keep, "w_q")
         x_by_d0 = held([P, R * PACK], BF16, "x_by_d0")
-        weave_x(x_by_d0, x_raw0, slice(0, R // 4), nc.vector.tensor_copy)
-        targets0 = [scaled_targets(0, t, y_raw0, place_bank[t]) for t in range(PACK)]
-        x_q0 = quantized(x_by_d0[:], R, E4M3, keep, "x_q")
-        ws_q = quantized(w_by_slot[:], B * D, E4M3, keep, "ws_q", "x_by_d0")
+        for rows in halves:
+            weave_x(x_by_d0, x_raw0, rows, nc.vector.tensor_copy)
+        targets0 = [scaled_targets(0, t, y_raw0) for t in range(PACK)]
+        x_q0 = packed(R, keep, "x_q")
+        for rows in halves:
+            quantize(x_q0, rows, x_by_d0[:, rows.start * PACK : rows.stop * PACK], E4M3)
+        w_slot_q = quantized(w_by_slot[:], B * D, E4M3, keep, "w_slot_q", "x_by_d0")
         weave_w(1, slice(2, PACK), nc.scalar.copy)
-        clipped0, diff0 = residuals(0, w_q0, x_q0, targets0)
+        clipped0, residual0 = residuals(0, w_q0, x_q0, targets0)
         w_q1 = quantized(w_by_d[1][:], N, E4M3, keep, "w_q")
-        clip(0, last, diff0, clipped0)
+        clip(0, LAST, residual0, clipped0, all_rows)
+
         x_by_d1 = held([P, R * PACK], BF16, "x_by_d1", "staged0")
-        weave_x(x_by_d1, x_raw1, slice(0, R // 4), nc.scalar.copy)
-        targets1 = [scaled_targets(1, t, y_raw1, place_bank[t]) for t in range(PACK)]
+        weave_x(x_by_d1, x_raw1, all_rows, nc.scalar.copy)
+        targets1 = [scaled_targets(1, t, y_raw1) for t in range(PACK)]
         x_q1 = quantized(x_by_d1[:], R, E4M3, keep, "x_q")
-        gradients(0, clipped0, ws_q, result_bank + result_bank)
-        clipped1, diff1 = residuals(1, w_q1, x_q1, targets1)
-        clip(1, last, diff1, clipped1)
-        gradients(1, clipped1, ws_q, place_bank)
+        gradients(0, clipped0, w_slot_q, result_bank + result_bank, 2 * P)
+
+        clipped1, residual1 = residuals(1, w_q1, x_q1, targets1)
+        for rows in halves:
+            clip(1, LAST, residual1, clipped1, rows)
+        gradients(1, clipped1, w_slot_q, place_bank, P)

@@ -42,15 +42,16 @@ def tile_attend_ghub_x_ts_kernel(tc, xT, wT, y, wt, ts, offs, out):
         offsets = keep.tile([P, B * LIST_COLS], U16, name="offsets")
         w_planes = wT.rearrange("(p j) t -> p j t", j=PACK)
         table = [held([P, T], F32, "table%d" % j, "staged%d" % j) for j in range(PACK)]
-        nc.sync.dma_start(table[0][:], w_planes[:, 0, :])
         nc.sync.dma_start(offsets[:], offs)
         ts_row = held([P, T], F32, "ts_row")
-        nc.gpsimd.memset(ts_row[:, : T // 2], 0.0)
-        nc.vector.memset(ts_row[:, T // 2 :], 0.0)
-        nc.sync.dma_start(ts_row[0:1, :], ts[0:1, :])
+        nc.sync.dma_start(ts_row[P - 1 : P, :], ts[0:1, :])
+        nc.gpsimd.memset(ts_row[0 : P - 1, : T // 2], 0.0)
+        nc.vector.memset(ts_row[0 : P - 1, T // 2 :], 0.0)
+        nc.sync.dma_start(table[0][:], w_planes[:, 0, :])
         wt_rows = held([P, P], F32, "wt_rows")
-        nc.gpsimd.memset(wt_rows[:], 0.0)
-        nc.sync.dma_start(wt_rows[0 : B * ROW_TILES, :], wt.rearrange("b (k m) o -> (b k) (m o)", m=P))
+        first_row = P - B * ROW_TILES
+        nc.gpsimd.memset(wt_rows[0:first_row, :], 0.0)
+        nc.sync.dma_start(wt_rows[first_row:P, :], wt.rearrange("b (k m) o -> (b k) (m o)", m=P))
         for j in range(1, PACK):
             nc.sync.dma_start(table[j][:], w_planes[:, j, :])
 
@@ -59,7 +60,7 @@ def tile_attend_ghub_x_ts_kernel(tc, xT, wT, y, wt, ts, offs, out):
 
         nc.tensor.transpose(weight_bank[0][:, 0:P], wt_rows[:], identity[:])
         wt_cols = held([P, B * ROW_TILES], F32, "wt_cols")
-        nc.scalar.copy(wt_cols[:], weight_bank[0][:, 0 : B * ROW_TILES])
+        nc.scalar.copy(wt_cols[:], weight_bank[0][:, first_row:P])
         for b in range(B):
             for k in range(ROW_TILES):
                 column = wt_cols[:, b * ROW_TILES + k : b * ROW_TILES + k + 1]
@@ -111,8 +112,8 @@ def tile_attend_ghub_x_ts_kernel(tc, xT, wT, y, wt, ts, offs, out):
             turned = place_bank[b][:].rearrange("p (t m) -> p t m", t=PACK)
             for t in range(PACK):
                 nc.tensor.transpose(turned[:, t, :], ts_listed[:, b * N + t : (b + 1) * N : PACK], identity[:])
-            nc.scalar.copy(ts_col[b], turned[:, :, 0])
-            nc.scalar.activation(ts_abs[b], turned[:, :, 0], ACT.Abs)
+            nc.scalar.copy(ts_col[b], turned[:, :, P - 1])
+            nc.scalar.activation(ts_abs[b], turned[:, :, P - 1], ACT.Abs)
             nc.gpsimd.tensor_tensor(ts_square[b], ts_col[b], ts_col[b], ALU.mult)
             nc.gpsimd.tensor_scalar(ts_minus_abs[b], ts_abs[b], -1.0, 0.0, ALU.mult, ALU.add)
 
@@ -157,8 +158,8 @@ def tile_attend_ghub_x_ts_kernel(tc, xT, wT, y, wt, ts, offs, out):
                 x_raw[:].rearrange("p j (c i) -> p c j i", i=QUAD)[:, quads],
             )
 
-        def scaled_targets(b, t, y_raw):
-            turned = place_bank[t][:].rearrange("p (c m) -> p c m", c=PACK)
+        def scaled_targets(b, t, y_raw, bank):
+            turned = bank[:].rearrange("p (c m) -> p c m", c=PACK)
             for c in range(PACK):
                 nc.tensor.transpose(turned[:, c, :], y_raw[:, c, t:N:PACK], identity[:])
             target = held([P, R], F32, "target%d_%d" % (b, t), "target%d" % t)
@@ -181,30 +182,36 @@ def tile_attend_ghub_x_ts_kernel(tc, xT, wT, y, wt, ts, offs, out):
                 ALU.max,
             )
 
-        def residuals(b, w_q, x_q, targets):
+        def scores(w_q, x_q, banks):
+            for t in range(PACK):
+                multiply(banks[t], w_q, slice(t * P, (t + 1) * P), E4M3, x_q, all_rows)
+
+        def residuals(b, targets, banks):
             clipped = held([P, PACK, R], F32, "clipped%d" % b)
             residual = []
             for t in range(PACK):
-                multiply(place_bank[t], w_q, slice(t * P, (t + 1) * P), E4M3, x_q, all_rows)
                 residual.append(ring.tile([P, R], F32, name="residual"))
                 nc.vector.scalar_tensor_tensor(
-                    residual[t][:], place_bank[t][:], ts_square[b][:, t : t + 1], targets[t][:], ALU.mult, ALU.subtract
+                    residual[t][:], banks[t][:], ts_square[b][:, t : t + 1], targets[t][:], ALU.mult, ALU.subtract
                 )
                 if t >= 1:
                     clip(b, t - 1, residual[t - 1], clipped, all_rows)
             return clipped, residual[LAST]
 
         def weigh(b, rows, clipped):
+            h = ring.tile([P, (rows.stop - rows.start) * PACK], BF16, name="h", align_bytes=64)
+            weigh_into(h[:], b, rows, clipped)
+            return h
+
+        def weigh_into(h, b, rows, clipped):
             count = rows.stop - rows.start
-            h = ring.tile([P, count * PACK], BF16, name="h", align_bytes=64)
             weights = weight_bank[b][:, rows].rearrange("p (c i) -> p c i", i=QUAD)
             nc.vector.tensor_tensor(
-                h[:].rearrange("p (c i t) -> p c t i", i=QUAD, t=PACK),
+                h.rearrange("p (c i t) -> p c t i", i=QUAD, t=PACK),
                 clipped[:, :, rows].rearrange("p t (c i) -> p c t i", i=QUAD),
                 weights.unsqueeze(2).to_broadcast([P, count // QUAD, PACK, QUAD]),
                 ALU.mult,
             )
-            return h
 
         def finish(b, rows, h, w_slot_q, banks):
             h_q = quantized(h[:], rows.stop - rows.start, E5M2, ring, "h")
@@ -248,28 +255,43 @@ def tile_attend_ghub_x_ts_kernel(tc, xT, wT, y, wt, ts, offs, out):
         x_raw0 = load_x(0, "staged1")
         x_raw1 = load_x(1, "staged2")
         y_raw1 = load_y(1, "staged3")
+        wt_shared = held([P, P], F32, "wt_shared")
+        nc.sync.dma_start(wt_shared[:], wt[0, R - P : R, 0].partition_broadcast(P))
 
         w_q0 = quantized(w_by_d[0][:], N, E4M3, keep, "w_q")
         x_by_d0 = held([P, R * PACK], BF16, "x_by_d0")
         for rows in halves:
             weave_x(x_by_d0, x_raw0, rows, nc.vector.tensor_copy)
-        targets0 = [scaled_targets(0, t, y_raw0) for t in range(PACK)]
+        targets0 = [scaled_targets(0, t, y_raw0, place_bank[t]) for t in range(PACK)]
         x_q0 = packed(R, keep, "x_q")
         for rows in halves:
             quantize(x_q0, rows, x_by_d0[:, rows.start * PACK : rows.stop * PACK], E4M3)
         w_slot_q = quantized(w_by_slot[:], B * D, E4M3, keep, "w_slot_q", "x_by_d0")
         weave_w(1, slice(2, PACK), nc.scalar.copy)
-        clipped0, residual0 = residuals(0, w_q0, x_q0, targets0)
+        scores(w_q0, x_q0, place_bank)
+        clipped0, residual0 = residuals(0, targets0, place_bank)
         w_q1 = quantized(w_by_d[1][:], N, E4M3, keep, "w_q")
         clip(0, LAST, residual0, clipped0, all_rows)
 
         x_by_d1 = held([P, R * PACK], BF16, "x_by_d1", "staged0")
         weave_x(x_by_d1, x_raw1, all_rows, nc.scalar.copy)
-        targets1 = [scaled_targets(1, t, y_raw1) for t in range(PACK)]
+        targets1 = [scaled_targets(1, t, y_raw1, (place_bank[:2] + result_bank)[t]) for t in range(PACK)]
         x_q1 = quantized(x_by_d1[:], R, E4M3, keep, "x_q")
-        gradients(0, clipped0, w_slot_q, result_bank + result_bank, 2 * P)
+        banks1 = place_bank[2:] + place_bank[:2]
+        scores(w_q1, x_q1, banks1)
+        h_first = weigh(0, halves[0], clipped0)
+        h_second = ring.tile([P, 2 * P * PACK], BF16, name="h", align_bytes=64)
+        nc.gpsimd.tensor_tensor(
+            h_second[:, P * PACK :].rearrange("p (r t) -> p r t", t=PACK),
+            clipped0[:, :, R - P : R].rearrange("p t r -> p r t"),
+            wt_shared[:].unsqueeze(2).to_broadcast([P, P, PACK]),
+            ALU.mult,
+        )
+        weigh_into(h_second[:, : P * PACK], 0, slice(2 * P, 3 * P), clipped0)
+        finish(0, halves[0], h_first, w_slot_q, result_bank + result_bank)
+        finish(0, halves[1], h_second, w_slot_q, result_bank + result_bank)
 
-        clipped1, residual1 = residuals(1, w_q1, x_q1, targets1)
+        clipped1, residual1 = residuals(1, targets1, banks1)
         for rows in halves:
             clip(1, LAST, residual1, clipped1, rows)
-        gradients(1, clipped1, w_slot_q, place_bank, P)
+        gradients(1, clipped1, w_slot_q, banks1, P)

@@ -92,7 +92,7 @@ def tile_attend_ghub_x_ts_kernel(tc, xT, wT, y, wt, ts, offs, out):
             nc.scalar.copy(by_slot[:, :, j, :, :], turned.rearrange("p b u m -> p b m u"))
 
         table0_bf16 = held([P, T], BF16, "table0_bf16")
-        nc.scalar.activation(table0_bf16[:], table[0][:], ACT.Copy)
+        nc.vector.tensor_copy(table0_bf16[:], table[0][:])
         for b in range(B):
             nc.scalar.activation(w_listed[b][:, 0:N], table0_bf16[:].indirect(group_offsets(b)), ACT.Copy)
 
@@ -266,7 +266,7 @@ def tile_attend_ghub_x_ts_kernel(tc, xT, wT, y, wt, ts, offs, out):
         x_q0 = packed(R, keep, "x_q")
         for rows in halves:
             quantize(x_q0, rows, x_by_d0[:, rows.start * PACK : rows.stop * PACK], E4M3)
-        w_slot_q = quantized(w_by_slot[:], B * D, E4M3, keep, "w_slot_q", "x_by_d0")
+        w_slot_q = quantized(w_by_slot[:], B * D, E4M3, keep, "w_slot_q", "staged1")
         weave_w(1, slice(2, PACK), nc.scalar.copy)
         scores(w_q0, x_q0, place_bank)
         clipped0, residual0 = residuals(0, targets0, place_bank)

@@ -78,8 +78,8 @@ def tile_attend_ghub_x_ts_kernel(tc, xT, wT, y, wt, ts, offs, out):
 
         def weave_w(b, planes, copy):
             copy(
-                w_by_d[b][:].rearrange("p (t c i j) -> p c j i t", t=PACK, i=2, j=PACK)[:, :, planes],
-                w_listed[b][:].rearrange("p (j c i t) -> p c j i t", j=PACK, i=2, t=PACK)[:, :, planes],
+                w_by_d[b][:].rearrange("p (t c i j) -> p c t i j", t=PACK, i=2, j=PACK)[:, :, :, :, planes],
+                w_listed[b][:].rearrange("p (j c i t) -> p c t i j", j=PACK, i=2, t=PACK)[:, :, :, :, planes],
             )
 
         def turn_plane(j, bank):

@@ -143,7 +143,7 @@ def tile_attend_ghub_x_ts_kernel(tc, xT, wT, y, wt, ts, offs, out):
 
         def load_y(b, tag):
             y_raw = held([P, PACK, N], F32, "y_raw%d" % b, tag)
-            nc.sync.dma_start(y_raw[:], y[b].rearrange("(p c) n -> p c n", c=PACK))
+            nc.sync.dma_start(y_raw[:], y[b].rearrange("(c p) n -> p c n", c=PACK))
             return y_raw
 
         def load_x(b, tag):
@@ -163,12 +163,7 @@ def tile_attend_ghub_x_ts_kernel(tc, xT, wT, y, wt, ts, offs, out):
             for c in range(PACK):
                 nc.tensor.transpose(turned[:, c, :], y_raw[:, c, t:N:PACK], identity[:])
             target = held([P, R], F32, "target%d_%d" % (b, t), "target%d" % t)
-            nc.scalar.activation(
-                target[:].rearrange("p (m c) -> p m c", c=PACK),
-                turned.rearrange("p c m -> p m c"),
-                ACT.Copy,
-                scale=ts_col[b][:, t : t + 1],
-            )
+            nc.scalar.activation(target[:], bank[:], ACT.Copy, scale=ts_col[b][:, t : t + 1])
             return target
 
         def clip(b, t, residual, clipped, rows):

@@ -93,8 +93,10 @@ def tile_attend_ghub_x_ts_kernel(tc, xT, wT, y, wt, ts, offs, out):
 
         table0_bf16 = held([P, T], BF16, "table0_bf16")
         nc.vector.tensor_copy(table0_bf16[:], table[0][:])
-        for b in range(B):
-            nc.scalar.activation(w_listed[b][:, 0:N], table0_bf16[:].indirect(group_offsets(b)), ACT.Copy)
+        half_list = LIST_COLS // 2
+        nc.vector.tensor_copy(w_listed[0][:, : N // 2], table[0][:].indirect(offsets[:, :half_list]))
+        nc.scalar.activation(w_listed[0][:, N // 2 : N], table0_bf16[:].indirect(offsets[:, half_list:LIST_COLS]), ACT.Copy)
+        nc.scalar.activation(w_listed[1][:, 0:N], table0_bf16[:].indirect(group_offsets(1)), ACT.Copy)
 
         ts_listed = held([P, B * N], F32, "ts_listed")
         nc.vector.tensor_copy(ts_listed[:], ts_row[:].indirect(offsets[:]))
@@ -208,8 +210,9 @@ def tile_attend_ghub_x_ts_kernel(tc, xT, wT, y, wt, ts, offs, out):
                 ALU.mult,
             )
 
-        def finish(b, rows, h, w_slot_q, banks):
-            h_q = quantized(h[:], rows.stop - rows.start, E5M2, ring, "h")
+        def finish(b, rows, h, w_slot_q, banks, tag=None):
+            pool, name = (keep, "h_late") if tag else (ring, "h")
+            h_q = quantized(h[:], rows.stop - rows.start, E5M2, pool, name, tag)
             for k in range(rows.start // P, rows.stop // P):
                 tile_rows = slice(k * P - rows.start, (k + 1) * P - rows.start)
                 multiply(banks[k], h_q, tile_rows, E5M2, w_slot_q, slice(b * D, (b + 1) * D))
@@ -284,9 +287,9 @@ def tile_attend_ghub_x_ts_kernel(tc, xT, wT, y, wt, ts, offs, out):
         )
         weigh_into(h_second[:, : P * PACK], 0, slice(2 * P, 3 * P), clipped0)
         finish(0, halves[0], h_first, w_slot_q, result_bank + result_bank)
-        finish(0, halves[1], h_second, w_slot_q, result_bank + result_bank)
 
         clipped1, residual1 = residuals(1, targets1, banks1)
+        finish(0, halves[1], h_second, w_slot_q, result_bank + result_bank, "target3")
         for rows in halves:
             clip(1, LAST, residual1, clipped1, rows)
         gradients(1, clipped1, w_slot_q, banks1, P)

@@ -23,6 +23,8 @@ LIST_COLS = N // 16
 ROW_TILES = R // P
 QUAD = 4
 GPSIMD_PLACES = 2
+GPSIMD_ROWS = 120
+VECTOR_SLOTS = N // 2
 
 
 def tile_attend_ghub_x_ts_kernel(tc, xT, wT, y, wt, ts, offs, out):
@@ -93,9 +95,11 @@ def tile_attend_ghub_x_ts_kernel(tc, xT, wT, y, wt, ts, offs, out):
 
         table0_bf16 = held([P, T], BF16, "table0_bf16")
         nc.vector.tensor_copy(table0_bf16[:], table[0][:])
-        half_list = LIST_COLS // 2
-        nc.vector.tensor_copy(w_listed[0][:, : N // 2], table[0][:].indirect(offsets[:, :half_list]))
-        nc.scalar.activation(w_listed[0][:, N // 2 : N], table0_bf16[:].indirect(offsets[:, half_list:LIST_COLS]), ACT.Copy)
+        list_cut = VECTOR_SLOTS // 16
+        nc.vector.tensor_copy(w_listed[0][:, :VECTOR_SLOTS], table[0][:].indirect(offsets[:, :list_cut]))
+        nc.scalar.activation(
+            w_listed[0][:, VECTOR_SLOTS:N], table0_bf16[:].indirect(offsets[:, list_cut:LIST_COLS]), ACT.Copy
+        )
         nc.scalar.activation(w_listed[1][:, 0:N], table0_bf16[:].indirect(group_offsets(1)), ACT.Copy)
 
         ts_listed = held([P, B * N], F32, "ts_listed")
@@ -195,12 +199,10 @@ def tile_attend_ghub_x_ts_kernel(tc, xT, wT, y, wt, ts, offs, out):
                     clip(b, t - 1, residual[t - 1], clipped, all_rows)
             return clipped, residual[LAST]
 
-        def weigh(b, rows, clipped):
-            h = ring.tile([P, (rows.stop - rows.start) * PACK], BF16, name="h", align_bytes=64)
-            weigh_into(h[:], b, rows, clipped)
-            return h
+        def h_tile(count):
+            return ring.tile([P, count * PACK], BF16, name="h", align_bytes=64)
 
-        def weigh_into(h, b, rows, clipped):
+        def weigh(h, b, rows, clipped):
             count = rows.stop - rows.start
             weights = weight_bank[b][:, rows].rearrange("p (c i) -> p c i", i=QUAD)
             nc.vector.tensor_tensor(
@@ -210,9 +212,8 @@ def tile_attend_ghub_x_ts_kernel(tc, xT, wT, y, wt, ts, offs, out):
                 ALU.mult,
             )
 
-        def finish(b, rows, h, w_slot_q, banks, tag=None):
-            pool, name = (keep, "h_late") if tag else (ring, "h")
-            h_q = quantized(h[:], rows.stop - rows.start, E5M2, pool, name, tag)
+        def finish(b, rows, h, h_q, w_slot_q, banks):
+            quantize(h_q, slice(0, rows.stop - rows.start), h[:], E5M2)
             for k in range(rows.start // P, rows.stop // P):
                 tile_rows = slice(k * P - rows.start, (k + 1) * P - rows.start)
                 multiply(banks[k], h_q, tile_rows, E5M2, w_slot_q, slice(b * D, (b + 1) * D))
@@ -229,15 +230,6 @@ def tile_attend_ghub_x_ts_kernel(tc, xT, wT, y, wt, ts, offs, out):
                     )
                     nc.sync.dma_start(out[b, k * P : (k + 1) * P, d_cols], result[:, d_cols])
 
-        def gradients(b, clipped, w_slot_q, banks, span):
-            spans = [slice(r, r + span) for r in range(0, R, span)]
-            hs = []
-            for i, rows in enumerate(spans):
-                hs.append(weigh(b, rows, clipped))
-                if i >= 1:
-                    finish(b, spans[i - 1], hs[i - 1], w_slot_q, banks)
-            finish(b, spans[-1], hs[-1], w_slot_q, banks)
-
         all_rows = slice(0, R)
         halves = [slice(0, R // 2), slice(R // 2, R)]
 
@@ -253,8 +245,9 @@ def tile_attend_ghub_x_ts_kernel(tc, xT, wT, y, wt, ts, offs, out):
         x_raw0 = load_x(0, "staged1")
         x_raw1 = load_x(1, "staged2")
         y_raw1 = load_y(1, "staged3")
-        wt_shared = held([P, P], F32, "wt_shared")
-        nc.sync.dma_start(wt_shared[:], wt[0, R - P : R, 0].partition_broadcast(P))
+        gpsimd_rows = slice(R - GPSIMD_ROWS, R)
+        wt_shared = held([P, GPSIMD_ROWS], F32, "wt_shared")
+        nc.sync.dma_start(wt_shared[:], wt[0, gpsimd_rows, 0].partition_broadcast(P))
 
         w_q0 = quantized(w_by_d[0][:], N, E4M3, keep, "w_q")
         x_by_d0 = held([P, R * PACK], BF16, "x_by_d0")
@@ -273,23 +266,36 @@ def tile_attend_ghub_x_ts_kernel(tc, xT, wT, y, wt, ts, offs, out):
 
         x_by_d1 = held([P, R * PACK], BF16, "x_by_d1", "staged0")
         weave_x(x_by_d1, x_raw1, all_rows, nc.scalar.copy)
-        targets1 = [scaled_targets(1, t, y_raw1, (place_bank[:2] + result_bank)[t]) for t in range(PACK)]
+        y_banks1 = place_bank[:2] + result_bank
+        targets1 = [scaled_targets(1, t, y_raw1, y_banks1[t]) for t in range(PACK)]
         x_q1 = quantized(x_by_d1[:], R, E4M3, keep, "x_q")
-        banks1 = place_bank[2:] + place_bank[:2]
-        scores(w_q1, x_q1, banks1)
-        h_first = weigh(0, halves[0], clipped0)
-        h_second = ring.tile([P, 2 * P * PACK], BF16, name="h", align_bytes=64)
+        score_banks1 = place_bank[2:] + place_bank[:2]
+        scores(w_q1, x_q1, score_banks1)
+
+        h_first = h_tile(R // 2)
+        weigh(h_first[:], 0, halves[0], clipped0)
+        h_second = h_tile(R // 2)
+        h_cut = (gpsimd_rows.start - R // 2) * PACK
         nc.gpsimd.tensor_tensor(
-            h_second[:, P * PACK :].rearrange("p (r t) -> p r t", t=PACK),
-            clipped0[:, :, R - P : R].rearrange("p t r -> p r t"),
-            wt_shared[:].unsqueeze(2).to_broadcast([P, P, PACK]),
+            h_second[:, h_cut:].rearrange("p (r t) -> p r t", t=PACK),
+            clipped0[:, :, gpsimd_rows].rearrange("p t r -> p r t"),
+            wt_shared[:].unsqueeze(2).to_broadcast([P, GPSIMD_ROWS, PACK]),
             ALU.mult,
         )
-        weigh_into(h_second[:, : P * PACK], 0, slice(2 * P, 3 * P), clipped0)
-        finish(0, halves[0], h_first, w_slot_q, result_bank + result_bank)
+        weigh(h_second[:, :h_cut], 0, slice(R // 2, gpsimd_rows.start), clipped0)
+        result_banks0 = result_bank + result_bank
+        finish(0, halves[0], h_first, packed(R // 2, ring, "h"), w_slot_q, result_banks0)
 
-        clipped1, residual1 = residuals(1, targets1, banks1)
-        finish(0, halves[1], h_second, w_slot_q, result_bank + result_bank, "target3")
+        clipped1, residual1 = residuals(1, targets1, score_banks1)
+        finish(0, halves[1], h_second, packed(R // 2, keep, "h_late", "target%d" % LAST), w_slot_q, result_banks0)
         for rows in halves:
             clip(1, LAST, residual1, clipped1, rows)
-        gradients(1, clipped1, w_slot_q, banks1, P)
+
+        row_tiles = [slice(r, r + P) for r in range(0, R, P)]
+        hs = []
+        for k, rows in enumerate(row_tiles):
+            hs.append(h_tile(P))
+            weigh(hs[k][:], 1, rows, clipped1)
+            if k >= 1:
+                finish(1, row_tiles[k - 1], hs[k - 1], packed(P, ring, "h"), w_slot_q, score_banks1)
+        finish(1, row_tiles[-1], hs[-1], packed(P, ring, "h"), w_slot_q, score_banks1)

@@ -24,7 +24,6 @@ ROW_TILES = R // P
 QUAD = 4
 GPSIMD_PLACES = 2
 GPSIMD_ROWS = 120
-VECTOR_SLOTS = N // 2
 
 
 def tile_attend_ghub_x_ts_kernel(tc, xT, wT, y, wt, ts, offs, out):
@@ -93,22 +92,16 @@ def tile_attend_ghub_x_ts_kernel(tc, xT, wT, y, wt, ts, offs, out):
             by_slot = w_by_slot[:].bitcast(F32).rearrange("p (b j m u) -> p b j m u", b=B, j=PACK, u=2)
             nc.scalar.copy(by_slot[:, :, j, :, :], turned.rearrange("p b u m -> p b m u"))
 
-        table0_bf16 = held([P, T], BF16, "table0_bf16")
-        nc.vector.tensor_copy(table0_bf16[:], table[0][:])
-        list_cut = VECTOR_SLOTS // 16
-        nc.vector.tensor_copy(w_listed[0][:, :VECTOR_SLOTS], table[0][:].indirect(offsets[:, :list_cut]))
-        nc.scalar.activation(
-            w_listed[0][:, VECTOR_SLOTS:N], table0_bf16[:].indirect(offsets[:, list_cut:LIST_COLS]), ACT.Copy
-        )
-        nc.scalar.activation(w_listed[1][:, 0:N], table0_bf16[:].indirect(group_offsets(1)), ACT.Copy)
+        gather_plane(0, 0)
+        nc.scalar.activation(w_listed[1][:, 0:N], table[0][:].indirect(group_offsets(1)), ACT.Copy)
 
         ts_listed = held([P, B * N], F32, "ts_listed")
         nc.vector.tensor_copy(ts_listed[:], ts_row[:].indirect(offsets[:]))
         for b in range(B):
             gather_plane(1, b)
-            weave_w(b, slice(0, 2), nc.scalar.copy)
+            weave_w(b, slice(0, 2), nc.gpsimd.tensor_copy if b else nc.scalar.copy)
 
-        ts_read = held([P, 2, B, PACK], F32, "ts_read", "table0_bf16")
+        ts_read = held([P, 2, B, PACK], F32, "ts_read")
         ts_made = held([P, 2, B, PACK], F32, "ts_made")
         ts_col = [ts_read[:, 0, b, :] for b in range(B)]
         ts_abs = [ts_read[:, 1, b, :] for b in range(B)]
@@ -147,10 +140,11 @@ def tile_attend_ghub_x_ts_kernel(tc, xT, wT, y, wt, ts, offs, out):
                 stop=True,
             )
 
-        def load_y(b, tag):
-            y_raw = held([P, PACK, N], F32, "y_raw%d" % b, tag)
-            nc.sync.dma_start(y_raw[:], y[b].rearrange("(c p) n -> p c n", c=PACK))
-            return y_raw
+        def load_y(b, rows, tag):
+            count = (rows.stop - rows.start) // P
+            y_raw = held([P, count, N], F32, "y_raw%d_%d" % (b, rows.start), tag)
+            nc.sync.dma_start(y_raw[:], y[b, rows, :].rearrange("(c p) n -> p c n", p=P))
+            return [y_raw[:, c, :] for c in range(count)]
 
         def load_x(b, tag):
             x_raw = held([P, PACK, R], F32, "x_raw%d" % b, tag)
@@ -167,7 +161,7 @@ def tile_attend_ghub_x_ts_kernel(tc, xT, wT, y, wt, ts, offs, out):
         def scaled_targets(b, t, y_raw, bank):
             turned = bank[:].rearrange("p (c m) -> p c m", c=PACK)
             for c in range(PACK):
-                nc.tensor.transpose(turned[:, c, :], y_raw[:, c, t:N:PACK], identity[:])
+                nc.tensor.transpose(turned[:, c, :], y_raw[c][:, t:N:PACK], identity[:])
             target = held([P, R], F32, "target%d_%d" % (b, t), "target%d" % t)
             nc.scalar.activation(target[:], bank[:], ACT.Copy, scale=ts_col[b][:, t : t + 1])
             return target
@@ -236,15 +230,19 @@ def tile_attend_ghub_x_ts_kernel(tc, xT, wT, y, wt, ts, offs, out):
         turn_plane(0, result_bank[0])
         turn_plane(1, result_bank[1])
         for j in range(2, PACK):
-            for b in range(B):
-                gather_plane(j, b)
-            turn_plane(j, place_bank[j])
+            gather_plane(j, 0)
+            if j < LAST:
+                gather_plane(j, 1)
+            else:
+                nc.scalar.activation(w_listed[1][:, j * N :], table[j][:].indirect(group_offsets(1)), ACT.Copy)
+            turn_plane(j, result_bank[j - 2])
         weave_w(0, slice(2, PACK), nc.vector.tensor_copy)
 
-        y_raw0 = load_y(0, "staged0")
-        x_raw0 = load_x(0, "staged1")
+        y_raw0 = load_y(0, halves[0], "ts_row")
+        x_raw0 = load_x(0, "staged0")
+        y_raw0.extend(load_y(0, halves[1], "staged1"))
         x_raw1 = load_x(1, "staged2")
-        y_raw1 = load_y(1, "staged3")
+        y_raw1 = load_y(1, all_rows, "staged3")
         gpsimd_rows = slice(R - GPSIMD_ROWS, R)
         wt_shared = held([P, GPSIMD_ROWS], F32, "wt_shared")
         nc.sync.dma_start(wt_shared[:], wt[0, gpsimd_rows, 0].partition_broadcast(P))
@@ -257,22 +255,23 @@ def tile_attend_ghub_x_ts_kernel(tc, xT, wT, y, wt, ts, offs, out):
         x_q0 = packed(R, keep, "x_q")
         for rows in halves:
             quantize(x_q0, rows, x_by_d0[:, rows.start * PACK : rows.stop * PACK], E4M3)
-        w_slot_q = quantized(w_by_slot[:], B * D, E4M3, keep, "w_slot_q", "staged1")
+        w_slot_q = quantized(w_by_slot[:], B * D, E4M3, keep, "w_slot_q", "staged0")
         weave_w(1, slice(2, PACK), nc.scalar.copy)
-        scores(w_q0, x_q0, place_bank)
-        clipped0, residual0 = residuals(0, targets0, place_bank)
+        score_banks0 = result_bank + place_bank[:2]
+        scores(w_q0, x_q0, score_banks0)
+        clipped0, residual0 = residuals(0, targets0, score_banks0)
         w_q1 = quantized(w_by_d[1][:], N, E4M3, keep, "w_q")
         clip(0, LAST, residual0, clipped0, all_rows)
 
-        x_by_d1 = held([P, R * PACK], BF16, "x_by_d1", "staged0")
+        x_by_d1 = held([P, R * PACK], BF16, "x_by_d1", "staged1")
         weave_x(x_by_d1, x_raw1, all_rows, nc.scalar.copy)
-        y_banks1 = place_bank[:2] + result_bank
+        y_banks1 = place_bank[2:] + result_bank
         targets1 = [scaled_targets(1, t, y_raw1, y_banks1[t]) for t in range(PACK)]
         x_q1 = quantized(x_by_d1[:], R, E4M3, keep, "x_q")
-        score_banks1 = place_bank[2:] + place_bank[:2]
+        score_banks1 = place_bank
         scores(w_q1, x_q1, score_banks1)
 
-        h_first = h_tile(R // 2)
+        h_first = held([P, R // 2 * PACK], BF16, "h_first", "staged2")
         weigh(h_first[:], 0, halves[0], clipped0)
         h_second = h_tile(R // 2)
         h_cut = (gpsimd_rows.start - R // 2) * PACK

@@ -99,7 +99,15 @@ def tile_attend_ghub_x_ts_kernel(tc, xT, wT, y, wt, ts, offs, out):
         nc.vector.tensor_copy(ts_listed[:], ts_row[:].indirect(offsets[:]))
         for b in range(B):
             gather_plane(1, b)
-            weave_w(b, slice(0, 2), nc.gpsimd.tensor_copy if b else nc.scalar.copy)
+        weave_w(0, slice(0, 2), nc.scalar.copy)
+        nc.gpsimd.tensor_scalar(
+            w_by_d[1][:].rearrange("p (t m j) -> p t m j", t=PACK, j=PACK)[:, :, :, 0:2],
+            w_listed[1][:].rearrange("p (j m t) -> p t m j", j=PACK, t=PACK)[:, :, :, 0:2],
+            1.0,
+            0.0,
+            ALU.mult,
+            ALU.add,
+        )
 
         ts_read = held([P, 2, B, PACK], F32, "ts_read")
         ts_made = held([P, 2, B, PACK], F32, "ts_made")

@@ -154,24 +154,23 @@ def tile_attend_ghub_x_ts_kernel(tc, xT, wT, y, wt, ts, offs, out):
             nc.sync.dma_start(y_raw[:], y[b, rows, :].rearrange("(c p) n -> p c n", p=P))
             return [y_raw[:, c, :] for c in range(count)]
 
-        def load_x(b, tag):
-            x_raw = held([P, PACK, R], F32, "x_raw%d" % b, tag)
-            nc.sync.dma_start(x_raw[:], xT[b].rearrange("(p j) r -> p j r", j=PACK))
+        def load_x(b, rows, tag):
+            x_raw = held([P, PACK, rows.stop - rows.start], F32, "x_raw%d_%d" % (b, rows.start), tag)
+            nc.sync.dma_start(x_raw[:], xT[b].rearrange("(p j) r -> p j r", j=PACK)[:, :, rows])
             return x_raw
 
         def weave_x(x_by_d, x_raw, rows, copy):
             quads = slice(rows.start // QUAD, rows.stop // QUAD)
             copy(
                 x_by_d[:].rearrange("p (c i j) -> p c j i", i=QUAD, j=PACK)[:, quads],
-                x_raw[:].rearrange("p j (c i) -> p c j i", i=QUAD)[:, quads],
+                x_raw.rearrange("p j (c i) -> p c j i", i=QUAD),
             )
 
-        def scaled_targets(b, t, y_raw, bank):
+        def scaled_targets(target, b, t, y_raw, bank):
             turned = bank[:].rearrange("p (c m) -> p c m", c=PACK)
             for c in range(PACK):
                 nc.tensor.transpose(turned[:, c, :], y_raw[c][:, t:N:PACK], identity[:])
-            target = held([P, R], F32, "target%d_%d" % (b, t), "target%d" % t)
-            nc.scalar.activation(target[:], bank[:], ACT.Copy, scale=ts_col[b][:, t : t + 1])
+            nc.scalar.activation(target, bank[:], ACT.Copy, scale=ts_col[b][:, t : t + 1])
             return target
 
         def clip(b, t, residual, clipped, rows):
@@ -195,7 +194,7 @@ def tile_attend_ghub_x_ts_kernel(tc, xT, wT, y, wt, ts, offs, out):
             for t in range(PACK):
                 residual.append(ring.tile([P, R], F32, name="residual"))
                 nc.vector.scalar_tensor_tensor(
-                    residual[t][:], banks[t][:], ts_square[b][:, t : t + 1], targets[t][:], ALU.mult, ALU.subtract
+                    residual[t][:], banks[t][:], ts_square[b][:, t : t + 1], targets[t], ALU.mult, ALU.subtract
                 )
                 if t >= 1:
                     clip(b, t - 1, residual[t - 1], clipped, all_rows)
@@ -247,10 +246,10 @@ def tile_attend_ghub_x_ts_kernel(tc, xT, wT, y, wt, ts, offs, out):
         weave_w(0, slice(2, PACK), nc.vector.tensor_copy)
 
         y_raw0 = load_y(0, halves[0], "ts_row")
-        x_raw0 = load_x(0, "staged0")
+        x_raw0 = load_x(0, all_rows, "staged0")
         y_raw0.extend(load_y(0, halves[1], "staged1"))
-        x_raw1 = load_x(1, "staged2")
-        y_raw1 = load_y(1, all_rows, "staged3")
+        y_raw1 = load_y(1, all_rows, "staged2")
+        x_raw1 = [load_x(1, rows, tag) for rows, tag in zip(halves, ("staged3", "w_listed0"))]
         gpsimd_rows = slice(R - GPSIMD_ROWS, R)
         wt_shared = held([P, GPSIMD_ROWS], F32, "wt_shared")
         nc.sync.dma_start(wt_shared[:], wt[0, gpsimd_rows, 0].partition_broadcast(P))
@@ -258,8 +257,9 @@ def tile_attend_ghub_x_ts_kernel(tc, xT, wT, y, wt, ts, offs, out):
         w_q0 = quantized(w_by_d[0][:], N, E4M3, keep, "w_q")
         x_by_d0 = held([P, R * PACK], BF16, "x_by_d0")
         for rows in halves:
-            weave_x(x_by_d0, x_raw0, rows, nc.vector.tensor_copy)
-        targets0 = [scaled_targets(0, t, y_raw0, place_bank[t]) for t in range(PACK)]
+            weave_x(x_by_d0, x_raw0[:, :, rows], rows, nc.vector.tensor_copy)
+        early = held([P, PACK, R], F32, "targets0")
+        targets0 = [scaled_targets(early[:, t, :], 0, t, y_raw0, place_bank[t]) for t in range(PACK)]
         x_q0 = packed(R, keep, "x_q")
         for rows in halves:
             quantize(x_q0, rows, x_by_d0[:, rows.start * PACK : rows.stop * PACK], E4M3)
@@ -272,14 +272,16 @@ def tile_attend_ghub_x_ts_kernel(tc, xT, wT, y, wt, ts, offs, out):
         clip(0, LAST, residual0, clipped0, all_rows)
 
         x_by_d1 = held([P, R * PACK], BF16, "x_by_d1", "staged1")
-        weave_x(x_by_d1, x_raw1, all_rows, nc.scalar.copy)
+        for i, rows in enumerate(halves):
+            weave_x(x_by_d1, x_raw1[i][:], rows, nc.scalar.copy)
         y_banks1 = place_bank[2:] + result_bank
-        targets1 = [scaled_targets(1, t, y_raw1, y_banks1[t]) for t in range(PACK)]
+        late = held([P, PACK, R], F32, "targets1", "staged3")
+        targets1 = [scaled_targets(late[:, t, :], 1, t, y_raw1, y_banks1[t]) for t in range(PACK)]
         x_q1 = quantized(x_by_d1[:], R, E4M3, keep, "x_q")
         score_banks1 = place_bank
         scores(w_q1, x_q1, score_banks1)
 
-        h_first = held([P, R // 2 * PACK], BF16, "h_first", "staged2")
+        h_first = held([P, R // 2 * PACK], BF16, "h_first", "w_listed0")
         weigh(h_first[:], 0, halves[0], clipped0)
         h_second = h_tile(R // 2)
         h_cut = (gpsimd_rows.start - R // 2) * PACK
@@ -294,7 +296,7 @@ def tile_attend_ghub_x_ts_kernel(tc, xT, wT, y, wt, ts, offs, out):
         finish(0, halves[0], h_first, packed(R // 2, ring, "h"), w_slot_q, result_banks0)
 
         clipped1, residual1 = residuals(1, targets1, score_banks1)
-        finish(0, halves[1], h_second, packed(R // 2, keep, "h_late", "target%d" % LAST), w_slot_q, result_banks0)
+        finish(0, halves[1], h_second, packed(R // 2, keep, "h_late", "staged3"), w_slot_q, result_banks0)
         for rows in halves:
             clip(1, LAST, residual1, clipped1, rows)
 

@@ -251,7 +251,7 @@ def tile_attend_ghub_x_ts_kernel(tc, xT, wT, y, wt, ts, offs, out):
         y_raw1 = load_y(1, all_rows, "staged2")
         x_raw1 = [load_x(1, rows, tag) for rows, tag in zip(halves, ("staged3", "w_listed0"))]
         gpsimd_rows = slice(R - GPSIMD_ROWS, R)
-        wt_shared = held([P, GPSIMD_ROWS], F32, "wt_shared")
+        wt_shared = held([P, GPSIMD_ROWS], F32, "wt_shared", "w_listed1")
         nc.sync.dma_start(wt_shared[:], wt[0, gpsimd_rows, 0].partition_broadcast(P))
 
         w_q0 = quantized(w_by_d[0][:], N, E4M3, keep, "w_q")

@@ -71,43 +71,47 @@ def tile_attend_ghub_x_ts_kernel(tc, xT, wT, y, wt, ts, offs, out):
             return offsets[:, b * LIST_COLS : (b + 1) * LIST_COLS]
 
         w_listed = [held([P, PACK * N], BF16, "w_listed%d" % b) for b in range(B)]
+        room = [[1, 2, 0, 1], [0, 1, 2, 3]]
+
+        def plane(b, j, count=1):
+            return w_listed[b][:, room[b][j] * N : (room[b][j] + count) * N]
         w_by_slot = held([P, B * D * PACK], BF16, "w_by_slot")
         w_by_d = [held([P, N * PACK], BF16, "w_by_d%d" % b) for b in range(B)]
 
         def gather_plane(j, b):
-            nc.vector.tensor_copy(w_listed[b][:, j * N : (j + 1) * N], table[j][:].indirect(group_offsets(b)))
+            nc.vector.tensor_copy(plane(b, j), table[j][:].indirect(group_offsets(b)))
 
         def weave_w(b, planes, copy):
             copy(
                 w_by_d[b][:].rearrange("p (t c i j) -> p c t i j", t=PACK, i=2, j=PACK)[:, :, :, :, planes],
-                w_listed[b][:].rearrange("p (j c i t) -> p c t i j", j=PACK, i=2, t=PACK)[:, :, :, :, planes],
+                plane(b, planes.start, 2).rearrange("p (j c i t) -> p c t i j", j=2, i=2, t=PACK),
             )
 
         def turn_plane(j, bank):
             turned = bank[:].rearrange("p (b u m) -> p b u m", b=B, u=2)
             for b in range(B):
-                words = w_listed[b][:, j * N : (j + 1) * N].bitcast(F32)
+                words = plane(b, j).bitcast(F32)
                 for u in range(2):
                     nc.tensor.transpose(turned[:, b, u, :], words[:, u : N // 2 : 2], identity[:])
             by_slot = w_by_slot[:].bitcast(F32).rearrange("p (b j m u) -> p b j m u", b=B, j=PACK, u=2)
             nc.scalar.copy(by_slot[:, :, j, :, :], turned.rearrange("p b u m -> p b m u"))
 
-        gather_plane(0, 0)
-        nc.scalar.activation(w_listed[1][:, 0:N], table[0][:].indirect(group_offsets(1)), ACT.Copy)
+        for b in range(B):
+            gather_plane(0, b)
 
         ts_listed = held([P, B * N], F32, "ts_listed")
         nc.vector.tensor_copy(ts_listed[:], ts_row[:].indirect(offsets[:]))
         for b in range(B):
             gather_plane(1, b)
-        weave_w(0, slice(0, 2), nc.scalar.copy)
-        nc.gpsimd.tensor_scalar(
-            w_by_d[1][:].rearrange("p (t m j) -> p t m j", t=PACK, j=PACK)[:, :, :, 0:2],
-            w_listed[1][:].rearrange("p (j m t) -> p t m j", j=PACK, t=PACK)[:, :, :, 0:2],
-            1.0,
-            0.0,
-            ALU.mult,
-            ALU.add,
-        )
+        for b in range(B):
+            nc.gpsimd.tensor_scalar(
+                w_by_d[b][:].rearrange("p (t m j) -> p t m j", t=PACK, j=PACK)[:, :, :, 0:2],
+                plane(b, 0, 2).rearrange("p (j m t) -> p t m j", j=2, t=PACK),
+                1.0,
+                0.0,
+                ALU.mult,
+                ALU.add,
+            )
 
         ts_read = held([P, 2, B, PACK], F32, "ts_read")
         ts_made = held([P, 2, B, PACK], F32, "ts_made")
@@ -238,10 +242,7 @@ def tile_attend_ghub_x_ts_kernel(tc, xT, wT, y, wt, ts, offs, out):
         turn_plane(1, result_bank[1])
         for j in range(2, PACK):
             gather_plane(j, 0)
-            if j < LAST:
-                gather_plane(j, 1)
-            else:
-                nc.scalar.activation(w_listed[1][:, j * N :], table[j][:].indirect(group_offsets(1)), ACT.Copy)
+            nc.scalar.activation(plane(1, j), table[j][:].indirect(group_offsets(1)), ACT.Copy)
             turn_plane(j, result_bank[j - 2])
         weave_w(0, slice(2, PACK), nc.vector.tensor_copy)
 

@@ -62,10 +62,13 @@ def tile_attend_ghub_x_ts_kernel(tc, xT, wT, y, wt, ts, offs, out):
         nc.tensor.transpose(weight_bank[0][:, 0:P], wt_rows[:], identity[:])
         wt_cols = held([P, B * ROW_TILES], F32, "wt_cols")
         nc.scalar.copy(wt_cols[:], weight_bank[0][:, first_row:P])
-        for b in range(B):
+
+        def spread_weights(b):
             for k in range(ROW_TILES):
                 column = wt_cols[:, b * ROW_TILES + k : b * ROW_TILES + k + 1]
                 nc.tensor.transpose(weight_bank[b][:, k * P : (k + 1) * P], column.to_broadcast([P, P]), identity[:])
+
+        spread_weights(0)
 
         def group_offsets(b):
             return offsets[:, b * LIST_COLS : (b + 1) * LIST_COLS]
@@ -75,7 +78,6 @@ def tile_attend_ghub_x_ts_kernel(tc, xT, wT, y, wt, ts, offs, out):
 
         def plane(b, j, count=1):
             return w_listed[b][:, room[b][j] * N : (room[b][j] + count) * N]
-        w_by_slot = held([P, B * D * PACK], BF16, "w_by_slot")
         w_by_d = [held([P, N * PACK], BF16, "w_by_d%d" % b) for b in range(B)]
 
         def gather_plane(j, b):
@@ -87,14 +89,18 @@ def tile_attend_ghub_x_ts_kernel(tc, xT, wT, y, wt, ts, offs, out):
                 plane(b, planes.start, 2).rearrange("p (j c i t) -> p c t i j", j=2, i=2, t=PACK),
             )
 
-        def turn_plane(j, bank):
-            turned = bank[:].rearrange("p (b u m) -> p b u m", b=B, u=2)
-            for b in range(B):
-                words = plane(b, j).bitcast(F32)
-                for u in range(2):
-                    nc.tensor.transpose(turned[:, b, u, :], words[:, u : N // 2 : 2], identity[:])
-            by_slot = w_by_slot[:].bitcast(F32).rearrange("p (b j m u) -> p b j m u", b=B, j=PACK, u=2)
-            nc.scalar.copy(by_slot[:, :, j, :, :], turned.rearrange("p b u m -> p b m u"))
+        def turn(b, j, bank, half):
+            words = plane(b, j).bitcast(F32)
+            for u in range(2):
+                nc.tensor.transpose(bank[:, (2 * half + u) * P : (2 * half + u + 1) * P], words[:, u : N // 2 : 2], identity[:])
+
+        def lay(bank, first, second):
+            rooms = [b * PACK + j for b, j in (first, second)]
+            by_slot = w_by_slot[:].bitcast(F32).rearrange("p (k m u) -> p k m u", m=P, u=2)
+            nc.scalar.copy(
+                by_slot[:, rooms[0] : rooms[1] + 1 : rooms[1] - rooms[0]],
+                bank[:].rearrange("p (k u m) -> p k m u", k=2, u=2),
+            )
 
         for b in range(B):
             gather_plane(0, b)
@@ -125,8 +131,8 @@ def tile_attend_ghub_x_ts_kernel(tc, xT, wT, y, wt, ts, offs, out):
                 nc.tensor.transpose(turned[:, t, :], ts_listed[:, b * N + t : (b + 1) * N : PACK], identity[:])
             nc.scalar.copy(ts_col[b], turned[:, :, P - 1])
             nc.scalar.activation(ts_abs[b], turned[:, :, P - 1], ACT.Abs)
-            nc.gpsimd.tensor_tensor(ts_square[b], ts_col[b], ts_col[b], ALU.mult)
-            nc.gpsimd.tensor_scalar(ts_minus_abs[b], ts_abs[b], -1.0, 0.0, ALU.mult, ALU.add)
+            nc.scalar.activation(ts_square[b], turned[:, :, P - 1], ACT.Square)
+            nc.scalar.activation(ts_minus_abs[b], ts_abs[b], ACT.Copy, scale=-1.0)
 
         def packed(width, pool, name, tag=None):
             codes = pool.tile([P, width], U32, name=name + "_codes", tag=tag or name + "_codes", align_bytes=64)
@@ -238,51 +244,73 @@ def tile_attend_ghub_x_ts_kernel(tc, xT, wT, y, wt, ts, offs, out):
         all_rows = slice(0, R)
         halves = [slice(0, R // 2), slice(R // 2, R)]
 
-        turn_plane(0, result_bank[0])
-        turn_plane(1, result_bank[1])
-        for j in range(2, PACK):
-            gather_plane(j, 0)
-            nc.scalar.activation(plane(1, j), table[j][:].indirect(group_offsets(1)), ACT.Copy)
-            turn_plane(j, result_bank[j - 2])
+        w_by_slot = held([P, B * D * PACK], BF16, "w_by_slot")
+        for b in range(B):
+            turn(b, 0, result_bank[0], b)
+        lay(result_bank[0], (0, 0), (1, 0))
+        turn(0, 1, result_bank[1], 0)
+        turn(1, 1, weight_bank[1], 0)
+        gather_plane(2, 0)
+        nc.scalar.activation(plane(1, 2), table[2][:].indirect(group_offsets(1)), ACT.Copy)
+        turn(1, 2, weight_bank[1], 1)
+        lay(weight_bank[1], (1, 1), (1, 2))
+        gather_plane(LAST, 0)
+        nc.scalar.activation(plane(1, LAST), table[LAST][:].indirect(group_offsets(1)), ACT.Copy)
         weave_w(0, slice(2, PACK), nc.vector.tensor_copy)
+        weave_w(1, slice(2, PACK), nc.scalar.copy)
 
-        y_raw0 = load_y(0, halves[0], "ts_row")
-        x_raw0 = load_x(0, all_rows, "staged0")
-        y_raw0.extend(load_y(0, halves[1], "staged1"))
-        y_raw1 = load_y(1, all_rows, "staged2")
-        x_raw1 = [load_x(1, rows, tag) for rows, tag in zip(halves, ("staged3", "w_listed0"))]
+        y_raw0 = [load_y(0, slice(c * P, (c + 1) * P), None)[0] for c in range(2)]
+        x_raw0 = load_x(0, all_rows, "x0_last")
+        y_raw0.extend(load_y(0, slice(2 * P, LAST * P), None))
+        y_raw0.extend(load_y(0, slice(LAST * P, R), "y0_last"))
+        y_raw1 = load_y(1, all_rows, None)
+        x_raw1 = [load_x(1, rows, tag) for rows, tag in zip(halves, ("x1_first", "x1_last"))]
         gpsimd_rows = slice(R - GPSIMD_ROWS, R)
-        wt_shared = held([P, GPSIMD_ROWS], F32, "wt_shared", "w_listed1")
+        wt_shared = held([P, GPSIMD_ROWS], F32, "wt_shared")
         nc.sync.dma_start(wt_shared[:], wt[0, gpsimd_rows, 0].partition_broadcast(P))
 
         w_q0 = quantized(w_by_d[0][:], N, E4M3, keep, "w_q")
         x_by_d0 = held([P, R * PACK], BF16, "x_by_d0")
         for rows in halves:
             weave_x(x_by_d0, x_raw0[:, :, rows], rows, nc.vector.tensor_copy)
+        def turn_y0(tiles, places):
+            for c in tiles:
+                for t in places:
+                    nc.tensor.transpose(place_bank[t][:, c * P : (c + 1) * P], y_raw0[c][:, t:N:PACK], identity[:])
+
+        turn_y0(range(2), range(PACK))
+        turn(0, LAST, result_bank[1], 1)
+        lay(result_bank[1], (0, 1), (0, LAST))
+        turn(1, LAST, result_bank[0], 1)
+        turn(0, 2, result_bank[0], 0)
+        lay(result_bank[0], (0, 2), (1, LAST))
+        spread_weights(1)
+        turn_y0(range(2, ROW_TILES), range(PACK))
         early = held([P, PACK, R], F32, "targets0")
-        targets0 = [scaled_targets(early[:, t, :], 0, t, y_raw0, place_bank[t]) for t in range(PACK)]
+        targets0 = [early[:, t, :] for t in range(PACK)]
+        for t in range(PACK):
+            nc.scalar.activation(targets0[t], place_bank[t][:], ACT.Copy, scale=ts_col[0][:, t : t + 1])
         x_q0 = packed(R, keep, "x_q")
         for rows in halves:
             quantize(x_q0, rows, x_by_d0[:, rows.start * PACK : rows.stop * PACK], E4M3)
-        w_slot_q = quantized(w_by_slot[:], B * D, E4M3, keep, "w_slot_q", "staged0")
-        weave_w(1, slice(2, PACK), nc.scalar.copy)
+        w_slot_q = quantized(w_by_slot[:], B * D, E4M3, keep, "w_slot_q", "x0_last")
         score_banks0 = result_bank + place_bank[:2]
         scores(w_q0, x_q0, score_banks0)
         clipped0, residual0 = residuals(0, targets0, score_banks0)
         w_q1 = quantized(w_by_d[1][:], N, E4M3, keep, "w_q")
         clip(0, LAST, residual0, clipped0, all_rows)
 
-        x_by_d1 = held([P, R * PACK], BF16, "x_by_d1", "staged1")
+        x_by_d1 = held([P, R * PACK], BF16, "x_by_d1", "y0_last")
         for i, rows in enumerate(halves):
             weave_x(x_by_d1, x_raw1[i][:], rows, nc.scalar.copy)
         y_banks1 = place_bank[2:] + result_bank
-        late = held([P, PACK, R], F32, "targets1", "staged3")
+        late = held([P, PACK, R], F32, "targets1", "x1_first")
         targets1 = [scaled_targets(late[:, t, :], 1, t, y_raw1, y_banks1[t]) for t in range(PACK)]
         x_q1 = quantized(x_by_d1[:], R, E4M3, keep, "x_q")
         score_banks1 = place_bank
         scores(w_q1, x_q1, score_banks1)
 
-        h_first = held([P, R // 2 * PACK], BF16, "h_first", "w_listed0")
+        h_first = held([P, R // 2 * PACK], BF16, "h_first", "x1_last")
         weigh(h_first[:], 0, halves[0], clipped0)
         h_second = h_tile(R // 2)
         h_cut = (gpsimd_rows.start - R // 2) * PACK
@@ -297,7 +325,7 @@ def tile_attend_ghub_x_ts_kernel(tc, xT, wT, y, wt, ts, offs, out):
         finish(0, halves[0], h_first, packed(R // 2, ring, "h"), w_slot_q, result_banks0)
 
         clipped1, residual1 = residuals(1, targets1, score_banks1)
-        finish(0, halves[1], h_second, packed(R // 2, keep, "h_late", "staged3"), w_slot_q, result_banks0)
+        finish(0, halves[1], h_second, packed(R // 2, keep, "h_late", "x1_first"), w_slot_q, result_banks0)
         for rows in halves:
             clip(1, LAST, residual1, clipped1, rows)
 

@@ -31,6 +31,7 @@ def tile_attend_ghub_x_ts_kernel(tc, xT, wT, y, wt, ts, offs, out):
     with ExitStack() as ctx:
         keep = ctx.enter_context(tc.tile_pool(name="keep", bufs=1))
         ring = ctx.enter_context(tc.tile_pool(name="ring", bufs=ROW_TILES))
+        placed = ctx.enter_context(tc.tile_pool(name="placed", bufs=1))
         psum = ctx.enter_context(tc.psum_pool(name="psum", bufs=1))
 
         def held(shape, dtype, name, tag=None):
@@ -159,10 +160,9 @@ def tile_attend_ghub_x_ts_kernel(tc, xT, wT, y, wt, ts, offs, out):
             )
 
         def load_y(b, rows, tag):
-            count = (rows.stop - rows.start) // P
-            y_raw = held([P, count, N], F32, "y_raw%d_%d" % (b, rows.start), tag)
-            nc.sync.dma_start(y_raw[:], y[b, rows, :].rearrange("(c p) n -> p c n", p=P))
-            return [y_raw[:, c, :] for c in range(count)]
+            y_raw = held([P, 2, N], F32, "y_raw%d_%d" % (b, rows.start), tag)
+            nc.sync.dma_start(y_raw[:], y[b, rows, :].rearrange("(p c) n -> p c n", c=2))
+            return [y_raw[:, c, :] for c in range(2)]
 
         def load_x(b, rows, tag):
             x_raw = held([P, PACK, rows.stop - rows.start], F32, "x_raw%d_%d" % (b, rows.start), tag)
@@ -176,12 +176,20 @@ def tile_attend_ghub_x_ts_kernel(tc, xT, wT, y, wt, ts, offs, out):
                 x_raw.rearrange("p j (c i) -> p c j i", i=QUAD),
             )
 
+        def scale_out(target, b, t, bank):
+            nc.scalar.activation(
+                target.rearrange("p (h m c) -> p h m c", h=2, c=2),
+                bank[:].rearrange("p (h c m) -> p h m c", h=2, c=2),
+                ACT.Copy,
+                scale=ts_col[b][:, t : t + 1],
+            )
+            return target
+
         def scaled_targets(target, b, t, y_raw, bank):
             turned = bank[:].rearrange("p (c m) -> p c m", c=PACK)
             for c in range(PACK):
                 nc.tensor.transpose(turned[:, c, :], y_raw[c][:, t:N:PACK], identity[:])
-            nc.scalar.activation(target, bank[:], ACT.Copy, scale=ts_col[b][:, t : t + 1])
-            return target
+            return scale_out(target, b, t, bank)
 
         def clip(b, t, residual, clipped, rows):
             engine = nc.gpsimd if t < GPSIMD_PLACES else nc.vector
@@ -259,12 +267,12 @@ def tile_attend_ghub_x_ts_kernel(tc, xT, wT, y, wt, ts, offs, out):
         weave_w(0, slice(2, PACK), nc.vector.tensor_copy)
         weave_w(1, slice(2, PACK), nc.scalar.copy)
 
-        y_raw0 = [load_y(0, slice(c * P, (c + 1) * P), None)[0] for c in range(2)]
+        y_raw0 = load_y(0, halves[0], None)
         x_raw0 = load_x(0, all_rows, "x0_last")
-        y_raw0.extend(load_y(0, slice(2 * P, LAST * P), None))
-        y_raw0.extend(load_y(0, slice(LAST * P, R), "y0_last"))
-        y_raw1 = load_y(1, all_rows, None)
-        x_raw1 = [load_x(1, rows, tag) for rows, tag in zip(halves, ("x1_first", "x1_last"))]
+        y_raw0.extend(load_y(0, halves[1], "y0_last"))
+        x_raw1 = placed.tile([P, PACK, R], F32, name="x_raw1", offset=6144, align_bytes=64)
+        nc.sync.dma_start(x_raw1[:], xT[1].rearrange("(p j) r -> p j r", j=PACK))
+        y_raw1 = load_y(1, halves[0], None) + load_y(1, halves[1], None)
         gpsimd_rows = slice(R - GPSIMD_ROWS, R)
         wt_shared = held([P, GPSIMD_ROWS], F32, "wt_shared")
         nc.sync.dma_start(wt_shared[:], wt[0, gpsimd_rows, 0].partition_broadcast(P))
@@ -285,11 +293,12 @@ def tile_attend_ghub_x_ts_kernel(tc, xT, wT, y, wt, ts, offs, out):
         turn(0, 2, result_bank[0], 0)
         lay(result_bank[0], (0, 2), (1, LAST))
         spread_weights(1)
-        turn_y0(range(2, ROW_TILES), range(PACK))
+        for t in range(PACK):
+            turn_y0(range(2, ROW_TILES), [t])
         early = held([P, PACK, R], F32, "targets0")
         targets0 = [early[:, t, :] for t in range(PACK)]
         for t in range(PACK):
-            nc.scalar.activation(targets0[t], place_bank[t][:], ACT.Copy, scale=ts_col[0][:, t : t + 1])
+            scale_out(targets0[t], 0, t, place_bank[t])
         x_q0 = packed(R, keep, "x_q")
         for rows in halves:
             quantize(x_q0, rows, x_by_d0[:, rows.start * PACK : rows.stop * PACK], E4M3)
@@ -301,18 +310,17 @@ def tile_attend_ghub_x_ts_kernel(tc, xT, wT, y, wt, ts, offs, out):
         clip(0, LAST, residual0, clipped0, all_rows)
 
         x_by_d1 = held([P, R * PACK], BF16, "x_by_d1", "y0_last")
-        for i, rows in enumerate(halves):
-            weave_x(x_by_d1, x_raw1[i][:], rows, nc.scalar.copy)
+        weave_x(x_by_d1, x_raw1[:], all_rows, nc.scalar.copy)
         y_banks1 = place_bank[2:] + result_bank
-        late = held([P, PACK, R], F32, "targets1", "x1_first")
+        late = placed.tile([P, PACK, R], F32, name="targets1", offset=0, align_bytes=64)
         targets1 = [scaled_targets(late[:, t, :], 1, t, y_raw1, y_banks1[t]) for t in range(PACK)]
         x_q1 = quantized(x_by_d1[:], R, E4M3, keep, "x_q")
         score_banks1 = place_bank
         scores(w_q1, x_q1, score_banks1)
 
-        h_first = held([P, R // 2 * PACK], BF16, "h_first", "x1_last")
+        h_first = placed.tile([P, R // 2 * PACK], BF16, name="h_first", offset=8192, align_bytes=64)
         weigh(h_first[:], 0, halves[0], clipped0)
-        h_second = h_tile(R // 2)
+        h_second = held([P, R // 2 * PACK], BF16, "h_second", "y0_last")
         h_cut = (gpsimd_rows.start - R // 2) * PACK
         nc.gpsimd.tensor_tensor(
             h_second[:, h_cut:].rearrange("p (r t) -> p r t", t=PACK),
@@ -325,7 +333,9 @@ def tile_attend_ghub_x_ts_kernel(tc, xT, wT, y, wt, ts, offs, out):
         finish(0, halves[0], h_first, packed(R // 2, ring, "h"), w_slot_q, result_banks0)
 
         clipped1, residual1 = residuals(1, targets1, score_banks1)
-        finish(0, halves[1], h_second, packed(R // 2, keep, "h_late", "x1_first"), w_slot_q, result_banks0)
+        late_codes = placed.tile([P, R // 2], U32, name="late_codes", offset=6144, align_bytes=64)
+        late_scales = held([P, R // 2], U8, "late_scales")
+        finish(0, halves[1], h_second, (late_codes, late_scales), w_slot_q, result_banks0)
         for rows in halves:
             clip(1, LAST, residual1, clipped1, rows)
 

@@ -23,6 +23,7 @@ LIST_COLS = N // 16
 ROW_TILES = R // P
 QUAD = 4
 GPSIMD_PLACES = 2
+VECTOR_SLOTS = 160
 GPSIMD_ROWS = 120
 
 
@@ -95,12 +96,11 @@ def tile_attend_ghub_x_ts_kernel(tc, xT, wT, y, wt, ts, offs, out):
             for u in range(2):
                 nc.tensor.transpose(bank[:, (2 * half + u) * P : (2 * half + u + 1) * P], words[:, u : N // 2 : 2], identity[:])
 
-        def lay(bank, first, second):
-            rooms = [b * PACK + j for b, j in (first, second)]
-            by_slot = w_by_slot[:].bitcast(F32).rearrange("p (k m u) -> p k m u", m=P, u=2)
+        def lay(bank, groups, planes, halves_of_bank=slice(0, 2)):
+            by_slot = w_by_slot[:].bitcast(F32).rearrange("p (b h j m u) -> p b j h m u", b=B, h=2, j=PACK, u=2)
             nc.scalar.copy(
-                by_slot[:, rooms[0] : rooms[1] + 1 : rooms[1] - rooms[0]],
-                bank[:].rearrange("p (k u m) -> p k m u", k=2, u=2),
+                by_slot[:, groups, planes],
+                bank[:].rearrange("p (k u h m) -> p k h m u", k=2, u=2, h=2)[:, halves_of_bank],
             )
 
         for b in range(B):
@@ -150,7 +150,7 @@ def tile_attend_ghub_x_ts_kernel(tc, xT, wT, y, wt, ts, offs, out):
 
         def multiply(bank, stationary, m_cols, fmt, moving, n_cols):
             nc.tensor.matmul_mx(
-                out=bank[:],
+                out=bank,
                 lhsT=stationary[0][:, m_cols].bitcast(fmt),
                 lhsT_scale=stationary[1][:, m_cols],
                 rhs=moving[0][:, n_cols].bitcast(E4M3),
@@ -204,7 +204,7 @@ def tile_attend_ghub_x_ts_kernel(tc, xT, wT, y, wt, ts, offs, out):
 
         def scores(w_q, x_q, banks):
             for t in range(PACK):
-                multiply(banks[t], w_q, slice(t * P, (t + 1) * P), E4M3, x_q, all_rows)
+                multiply(banks[t][:], w_q, slice(t * P, (t + 1) * P), E4M3, x_q, all_rows)
 
         def residuals(b, targets, banks):
             clipped = held([P, PACK, R], F32, "clipped%d" % b)
@@ -235,17 +235,19 @@ def tile_attend_ghub_x_ts_kernel(tc, xT, wT, y, wt, ts, offs, out):
             quantize(h_q, slice(0, rows.stop - rows.start), h[:], E5M2)
             for k in range(rows.start // P, rows.stop // P):
                 tile_rows = slice(k * P - rows.start, (k + 1) * P - rows.start)
-                multiply(banks[k], h_q, tile_rows, E5M2, w_slot_q, slice(b * D, (b + 1) * D))
                 result = held([P, D], F32, "result%d_%d" % (b, k))
-                final = (b, k) == (B - 1, ROW_TILES - 1)
-                copy = nc.vector.tensor_copy if final else nc.scalar.copy
-                pieces = 2 if final else 1
-                for i in range(pieces):
-                    d_cols = slice(i * D // pieces, (i + 1) * D // pieces)
-                    m_cols = slice(i * P // pieces, (i + 1) * P // pieces)
+                if (b, k) == (B - 1, LAST):
+                    shares = [(banks[k], nc.vector.tensor_copy), (result_bank[0], nc.scalar.copy)]
+                else:
+                    shares = [(banks[k], nc.scalar.copy)]
+                width = D // len(shares)
+                for i, (bank, copy) in enumerate(shares):
+                    start = b * D + i * width
+                    multiply(bank[:, :width], h_q, tile_rows, E5M2, w_slot_q, slice(start, start + width))
+                    d_cols = slice(i * width, (i + 1) * width)
                     copy(
-                        result[:, d_cols].rearrange("p (m j) -> p m j", j=PACK),
-                        banks[k][:].rearrange("p (j m) -> p m j", j=PACK)[:, m_cols, :],
+                        result[:, d_cols].rearrange("p (h m j) -> p h m j", m=P // 2, j=PACK),
+                        bank[:, :width].rearrange("p (h j m) -> p h m j", j=PACK, m=P // 2),
                     )
                     nc.sync.dma_start(out[b, k * P : (k + 1) * P, d_cols], result[:, d_cols])
 
@@ -255,15 +257,17 @@ def tile_attend_ghub_x_ts_kernel(tc, xT, wT, y, wt, ts, offs, out):
         w_by_slot = held([P, B * D * PACK], BF16, "w_by_slot")
         for b in range(B):
             turn(b, 0, result_bank[0], b)
-        lay(result_bank[0], (0, 0), (1, 0))
+        lay(result_bank[0], slice(0, B), 0)
         turn(0, 1, result_bank[1], 0)
         turn(1, 1, weight_bank[1], 0)
         gather_plane(2, 0)
         nc.scalar.activation(plane(1, 2), table[2][:].indirect(group_offsets(1)), ACT.Copy)
         turn(1, 2, weight_bank[1], 1)
-        lay(weight_bank[1], (1, 1), (1, 2))
+        lay(weight_bank[1], 1, slice(1, 3))
         gather_plane(LAST, 0)
-        nc.scalar.activation(plane(1, LAST), table[LAST][:].indirect(group_offsets(1)), ACT.Copy)
+        cut = LIST_COLS + VECTOR_SLOTS // 16
+        nc.vector.tensor_copy(plane(1, LAST)[:, :VECTOR_SLOTS], table[LAST][:].indirect(offsets[:, LIST_COLS:cut]))
+        nc.scalar.activation(plane(1, LAST)[:, VECTOR_SLOTS:], table[LAST][:].indirect(offsets[:, cut:]), ACT.Copy)
         weave_w(0, slice(2, PACK), nc.vector.tensor_copy)
         weave_w(1, slice(2, PACK), nc.scalar.copy)
 
@@ -288,10 +292,11 @@ def tile_attend_ghub_x_ts_kernel(tc, xT, wT, y, wt, ts, offs, out):
 
         turn_y0(range(2), range(PACK))
         turn(0, LAST, result_bank[1], 1)
-        lay(result_bank[1], (0, 1), (0, LAST))
+        lay(result_bank[1], 0, slice(1, PACK, 2))
         turn(1, LAST, result_bank[0], 1)
         turn(0, 2, result_bank[0], 0)
-        lay(result_bank[0], (0, 2), (1, LAST))
+        lay(result_bank[0], 1, LAST, 1)
+        lay(result_bank[0], 0, 2, 0)
         spread_weights(1)
         for t in range(PACK):
             turn_y0(range(2, ROW_TILES), [t])
@@ -340,10 +345,12 @@ def tile_attend_ghub_x_ts_kernel(tc, xT, wT, y, wt, ts, offs, out):
             clip(1, LAST, residual1, clipped1, rows)
 
         row_tiles = [slice(r, r + P) for r in range(0, R, P)]
-        hs = []
-        for k, rows in enumerate(row_tiles):
-            hs.append(h_tile(P))
-            weigh(hs[k][:], 1, rows, clipped1)
+        hs = [held([P, P * PACK], BF16, "h1_%d" % k) for k in range(LAST)]
+        for k in range(LAST):
+            weigh(hs[k][:], 1, row_tiles[k], clipped1)
             if k >= 1:
                 finish(1, row_tiles[k - 1], hs[k - 1], packed(P, ring, "h"), w_slot_q, score_banks1)
-        finish(1, row_tiles[-1], hs[-1], packed(P, ring, "h"), w_slot_q, score_banks1)
+        finish(1, row_tiles[LAST - 1], hs[LAST - 1], packed(P, ring, "h"), w_slot_q, score_banks1)
+        h_last = held([P, P * PACK], BF16, "h_last", "h1_1")
+        weigh(h_last[:], 1, row_tiles[LAST], clipped1)
+        finish(1, row_tiles[LAST], h_last, packed(P, ring, "h"), w_slot_q, score_banks1)

@@ -273,7 +273,10 @@ def tile_attend_ghub_x_ts_kernel(tc, xT, wT, y, wt, ts, offs, out):
 
         y_raw0 = load_y(0, halves[0], None)
         x_raw0 = load_x(0, all_rows, "x0_last")
-        y_raw0.extend(load_y(0, halves[1], "y0_last"))
+        pairs_of_rows = y[0, halves[1], :].rearrange("(p c) n -> p c n", c=2)
+        for c, tag in enumerate((None, "y0_last")):
+            y_raw0.append(held([P, N], F32, "y_raw0_late%d" % c, tag))
+            nc.sync.dma_start(y_raw0[-1][:], pairs_of_rows[:, c, :])
         x_raw1 = placed.tile([P, PACK, R], F32, name="x_raw1", offset=6144, align_bytes=64)
         nc.sync.dma_start(x_raw1[:], xT[1].rearrange("(p j) r -> p j r", j=PACK))
         y_raw1 = load_y(1, halves[0], None) + load_y(1, halves[1], None)

@@ -107,7 +107,8 @@ def tile_attend_ghub_x_ts_kernel(tc, xT, wT, y, wt, ts, offs, out):
             gather_plane(0, b)
 
         ts_listed = held([P, B * N], F32, "ts_listed")
-        nc.vector.tensor_copy(ts_listed[:], ts_row[:].indirect(offsets[:]))
+        nc.vector.tensor_copy(ts_listed[:, :N], ts_row[:].indirect(group_offsets(0)))
+        nc.scalar.activation(ts_listed[:, N:], ts_row[:].indirect(group_offsets(1)), ACT.Copy)
         for b in range(B):
             gather_plane(1, b)
         for b in range(B):

@@ -71,6 +71,9 @@ def tile_attend_ghub_x_ts_kernel(tc, xT, wT, y, wt, ts, offs, out):
                 nc.tensor.transpose(weight_bank[b][:, k * P : (k + 1) * P], column.to_broadcast([P, P]), identity[:])
 
         spread_weights(0)
+        gpsimd_rows = slice(R - GPSIMD_ROWS, R)
+        wt_shared = held([P, GPSIMD_ROWS], F32, "wt_shared")
+        nc.scalar.copy(wt_shared[:], weight_bank[0][:, gpsimd_rows])
 
         def group_offsets(b):
             return offsets[:, b * LIST_COLS : (b + 1) * LIST_COLS]
@@ -281,9 +284,6 @@ def tile_attend_ghub_x_ts_kernel(tc, xT, wT, y, wt, ts, offs, out):
         x_raw1 = placed.tile([P, PACK, R], F32, name="x_raw1", offset=6144, align_bytes=64)
         nc.sync.dma_start(x_raw1[:], xT[1].rearrange("(p j) r -> p j r", j=PACK))
         y_raw1 = load_y(1, halves[0], None) + load_y(1, halves[1], None)
-        gpsimd_rows = slice(R - GPSIMD_ROWS, R)
-        wt_shared = held([P, GPSIMD_ROWS], F32, "wt_shared")
-        nc.sync.dma_start(wt_shared[:], wt[0, gpsimd_rows, 0].partition_broadcast(P))
 
         w_q0 = quantized(w_by_d[0][:], N, E4M3, keep, "w_q")
         x_by_d0 = held([P, R * PACK], BF16, "x_by_d0")

@@ -88,10 +88,15 @@ def tile_attend_ghub_x_ts_kernel(tc, xT, wT, y, wt, ts, offs, out):
         def gather_plane(j, b):
             nc.vector.tensor_copy(plane(b, j), table[j][:].indirect(group_offsets(b)))
 
-        def weave_w(b, planes, copy):
+        def gather_shared(j, slots):
+            cut = LIST_COLS + slots // 16
+            nc.vector.tensor_copy(plane(1, j)[:, :slots], table[j][:].indirect(offsets[:, LIST_COLS:cut]))
+            nc.scalar.activation(plane(1, j)[:, slots:], table[j][:].indirect(offsets[:, cut:]), ACT.Copy)
+
+        def weave_w(b, planes, copy, places=slice(0, PACK)):
             copy(
-                w_by_d[b][:].rearrange("p (t c i j) -> p c t i j", t=PACK, i=2, j=PACK)[:, :, :, :, planes],
-                plane(b, planes.start, 2).rearrange("p (j c i t) -> p c t i j", j=2, i=2, t=PACK),
+                w_by_d[b][:].rearrange("p (t c i j) -> p c t i j", t=PACK, i=2, j=PACK)[:, :, places, :, planes],
+                plane(b, planes.start, 2).rearrange("p (j c i t) -> p c t i j", j=2, i=2, t=PACK)[:, :, places],
             )
 
         def turn(b, j, bank, half):
@@ -112,8 +117,8 @@ def tile_attend_ghub_x_ts_kernel(tc, xT, wT, y, wt, ts, offs, out):
         ts_listed = held([P, B * N], F32, "ts_listed")
         nc.vector.tensor_copy(ts_listed[:, :N], ts_row[:].indirect(group_offsets(0)))
         nc.scalar.activation(ts_listed[:, N:], ts_row[:].indirect(group_offsets(1)), ACT.Copy)
-        for b in range(B):
-            gather_plane(1, b)
+        gather_plane(1, 0)
+        nc.scalar.activation(plane(1, 1), table[1][:].indirect(group_offsets(1)), ACT.Copy)
         for b in range(B):
             nc.gpsimd.tensor_scalar(
                 w_by_d[b][:].rearrange("p (t m j) -> p t m j", t=PACK, j=PACK)[:, :, :, 0:2],
@@ -236,7 +241,11 @@ def tile_attend_ghub_x_ts_kernel(tc, xT, wT, y, wt, ts, offs, out):
             )
 
         def finish(b, rows, h, h_q, w_slot_q, banks):
-            quantize(h_q, slice(0, rows.stop - rows.start), h[:], E5M2)
+            count = rows.stop - rows.start
+            parts = 2 if (b, rows.stop) == (B - 1, R) else 1
+            for i in range(parts):
+                columns = slice(i * count // parts, (i + 1) * count // parts)
+                quantize(h_q, columns, h[:, columns.start * PACK : columns.stop * PACK], E5M2)
             for k in range(rows.start // P, rows.stop // P):
                 tile_rows = slice(k * P - rows.start, (k + 1) * P - rows.start)
                 result = held([P, D], F32, "result%d_%d" % (b, k))
@@ -260,19 +269,18 @@ def tile_attend_ghub_x_ts_kernel(tc, xT, wT, y, wt, ts, offs, out):
 
         w_by_slot = held([P, B * D * PACK], BF16, "w_by_slot")
         for b in range(B):
-            turn(b, 0, result_bank[0], b)
-        lay(result_bank[0], slice(0, B), 0)
-        turn(0, 1, result_bank[1], 0)
-        turn(1, 1, weight_bank[1], 0)
+            for j in range(2):
+                turn(b, j, result_bank[b], j)
+            lay(result_bank[b], b, slice(0, 2))
+        spread_weights(1)
         gather_plane(2, 0)
-        nc.scalar.activation(plane(1, 2), table[2][:].indirect(group_offsets(1)), ACT.Copy)
-        turn(1, 2, weight_bank[1], 1)
-        lay(weight_bank[1], 1, slice(1, 3))
+        gather_shared(2, N // 2)
+        for b in range(B):
+            turn(b, 2, result_bank[b], 0)
         gather_plane(LAST, 0)
-        cut = LIST_COLS + VECTOR_SLOTS // 16
-        nc.vector.tensor_copy(plane(1, LAST)[:, :VECTOR_SLOTS], table[LAST][:].indirect(offsets[:, LIST_COLS:cut]))
-        nc.scalar.activation(plane(1, LAST)[:, VECTOR_SLOTS:], table[LAST][:].indirect(offsets[:, cut:]), ACT.Copy)
-        weave_w(0, slice(2, PACK), nc.vector.tensor_copy)
+        gather_shared(LAST, VECTOR_SLOTS)
+        for places in (slice(0, 2), slice(2, PACK)):
+            weave_w(0, slice(2, PACK), nc.vector.tensor_copy, places)
         weave_w(1, slice(2, PACK), nc.scalar.copy)
 
         y_raw0 = load_y(0, halves[0], None)
@@ -285,7 +293,9 @@ def tile_attend_ghub_x_ts_kernel(tc, xT, wT, y, wt, ts, offs, out):
         nc.sync.dma_start(x_raw1[:], xT[1].rearrange("(p j) r -> p j r", j=PACK))
         y_raw1 = load_y(1, halves[0], None) + load_y(1, halves[1], None)
 
-        w_q0 = quantized(w_by_d[0][:], N, E4M3, keep, "w_q")
+        w_q0 = packed(N, keep, "w_q")
+        for slots in halves:
+            quantize(w_q0, slots, w_by_d[0][:, slots.start * PACK : slots.stop * PACK], E4M3)
         x_by_d0 = held([P, R * PACK], BF16, "x_by_d0")
         for rows in halves:
             weave_x(x_by_d0, x_raw0[:, :, rows], rows, nc.vector.tensor_copy)
@@ -295,13 +305,9 @@ def tile_attend_ghub_x_ts_kernel(tc, xT, wT, y, wt, ts, offs, out):
                     nc.tensor.transpose(place_bank[t][:, c * P : (c + 1) * P], y_raw0[c][:, t:N:PACK], identity[:])
 
         turn_y0(range(2), range(PACK))
-        turn(0, LAST, result_bank[1], 1)
-        lay(result_bank[1], 0, slice(1, PACK, 2))
-        turn(1, LAST, result_bank[0], 1)
-        turn(0, 2, result_bank[0], 0)
-        lay(result_bank[0], 1, LAST, 1)
-        lay(result_bank[0], 0, 2, 0)
-        spread_weights(1)
+        for b in range(B):
+            turn(b, LAST, result_bank[b], 1)
+            lay(result_bank[b], b, slice(2, PACK))
         for t in range(PACK):
             turn_y0(range(2, ROW_TILES), [t])
         early = held([P, PACK, R], F32, "targets0")
@@ -332,9 +338,9 @@ def tile_attend_ghub_x_ts_kernel(tc, xT, wT, y, wt, ts, offs, out):
         h_second = held([P, R // 2 * PACK], BF16, "h_second", "y0_last")
         h_cut = (gpsimd_rows.start - R // 2) * PACK
         nc.gpsimd.tensor_tensor(
-            h_second[:, h_cut:].rearrange("p (r t) -> p r t", t=PACK),
-            clipped0[:, :, gpsimd_rows].rearrange("p t r -> p r t"),
-            wt_shared[:].unsqueeze(2).to_broadcast([P, GPSIMD_ROWS, PACK]),
+            h_second[:, h_cut:].rearrange("p (c i t) -> p c t i", i=QUAD, t=PACK),
+            clipped0[:, :, gpsimd_rows].rearrange("p t (c i) -> p c t i", i=QUAD),
+            wt_shared[:].rearrange("p (c i) -> p c i", i=QUAD).unsqueeze(2).to_broadcast([P, GPSIMD_ROWS // QUAD, PACK, QUAD]),
             ALU.mult,
         )
         weigh(h_second[:, :h_cut], 0, slice(R // 2, gpsimd_rows.start), clipped0)
@@ -356,5 +362,7 @@ def tile_attend_ghub_x_ts_kernel(tc, xT, wT, y, wt, ts, offs, out):
                 finish(1, row_tiles[k - 1], hs[k - 1], packed(P, ring, "h"), w_slot_q, score_banks1)
         finish(1, row_tiles[LAST - 1], hs[LAST - 1], packed(P, ring, "h"), w_slot_q, score_banks1)
         h_last = held([P, P * PACK], BF16, "h_last", "h1_1")
-        weigh(h_last[:], 1, row_tiles[LAST], clipped1)
+        for i in range(2):
+            rows = slice(R - P + i * P // 2, R - P + (i + 1) * P // 2)
+            weigh(h_last[:, i * P * 2 : (i + 1) * P * 2], 1, rows, clipped1)
         finish(1, row_tiles[LAST], h_last, packed(P, ring, "h"), w_slot_q, score_banks1)

@@ -23,7 +23,7 @@ LIST_COLS = N // 16
 ROW_TILES = R // P
 QUAD = 4
 GPSIMD_PLACES = 2
-VECTOR_SLOTS = 160
+VECTOR_SLOTS = 128
 GPSIMD_ROWS = 120
 
 
@@ -118,7 +118,7 @@ def tile_attend_ghub_x_ts_kernel(tc, xT, wT, y, wt, ts, offs, out):
         nc.vector.tensor_copy(ts_listed[:, :N], ts_row[:].indirect(group_offsets(0)))
         nc.scalar.activation(ts_listed[:, N:], ts_row[:].indirect(group_offsets(1)), ACT.Copy)
         gather_plane(1, 0)
-        nc.scalar.activation(plane(1, 1), table[1][:].indirect(group_offsets(1)), ACT.Copy)
+        gather_shared(1, N // 2)
         for b in range(B):
             nc.gpsimd.tensor_scalar(
                 w_by_d[b][:].rearrange("p (t m j) -> p t m j", t=PACK, j=PACK)[:, :, :, 0:2],

from contextlib import ExitStack

import concourse.mybir as mybir
from concourse.masks import make_identity

B, N, T, D, R = 2, 512, 2048, 512, 512
FLOPS = 2 * 2 * B * R * N * D

F32 = mybir.dt.float32
BF16 = mybir.dt.bfloat16
U32 = mybir.dt.uint32
U16 = mybir.dt.uint16
U8 = mybir.dt.uint8
E4M3 = mybir.dt.float8_e4m3fn_x4
E5M2 = mybir.dt.float8_e5m2_x4
ALU = mybir.AluOpType
ACT = mybir.ActivationFunctionType

P = 128
PACK = 4
LAST = PACK - 1
LIST_COLS = N // 16
ROW_TILES = R // P
QUAD = 4
GPSIMD_PLACES = 2
VECTOR_SLOTS = 128
GPSIMD_ROWS = 120


def tile_attend_ghub_x_ts_kernel(tc, xT, wT, y, wt, ts, offs, out):
    nc = tc.nc
    with ExitStack() as ctx:
        keep = ctx.enter_context(tc.tile_pool(name="keep", bufs=1))
        ring = ctx.enter_context(tc.tile_pool(name="ring", bufs=ROW_TILES))
        placed = ctx.enter_context(tc.tile_pool(name="placed", bufs=1))
        psum = ctx.enter_context(tc.psum_pool(name="psum", bufs=1))

        def held(shape, dtype, name, tag=None):
            return keep.tile(shape, dtype, name=name, tag=tag or name, align_bytes=64)

        weight_bank = [psum.tile([P, R], F32, name="weight_bank%d" % b) for b in range(B)]
        result_bank = [psum.tile([P, D], F32, name="result_bank%d" % i) for i in range(2)]
        place_bank = [psum.tile([P, R], F32, name="place_bank%d" % t) for t in range(PACK)]

        offsets = keep.tile([P, B * LIST_COLS], U16, name="offsets")
        w_planes = wT.rearrange("(p j) t -> p j t", j=PACK)
        table = [held([P, T], F32, "table%d" % j, "staged%d" % j) for j in range(PACK)]
        nc.sync.dma_start(offsets[:], offs)
        ts_row = held([P, T], F32, "ts_row")
        nc.sync.dma_start(ts_row[P - 1 : P, :], ts[0:1, :])
        nc.gpsimd.memset(ts_row[0 : P - 1, : T // 2], 0.0)
        nc.vector.memset(ts_row[0 : P - 1, T // 2 :], 0.0)
        nc.sync.dma_start(table[0][:], w_planes[:, 0, :])
        wt_rows = held([P, P], F32, "wt_rows")
        first_row = P - B * ROW_TILES
        nc.gpsimd.memset(wt_rows[0:first_row, :], 0.0)
        nc.sync.dma_start(wt_rows[first_row:P, :], wt.rearrange("b (k m) o -> (b k) (m o)", m=P))
        for j in range(1, PACK):
            nc.sync.dma_start(table[j][:], w_planes[:, j, :])

        identity = held([P, P], F32, "identity")
        make_identity(nc, identity[:])

        nc.tensor.transpose(weight_bank[0][:, 0:P], wt_rows[:], identity[:])
        wt_cols = held([P, B * ROW_TILES], F32, "wt_cols")
        nc.scalar.copy(wt_cols[:], weight_bank[0][:, first_row:P])

        def spread_weights(b):
            for k in range(ROW_TILES):
                column = wt_cols[:, b * ROW_TILES + k : b * ROW_TILES + k + 1]
                nc.tensor.transpose(weight_bank[b][:, k * P : (k + 1) * P], column.to_broadcast([P, P]), identity[:])

        spread_weights(0)
        gpsimd_rows = slice(R - GPSIMD_ROWS, R)
        wt_shared = held([P, GPSIMD_ROWS], F32, "wt_shared")
        nc.scalar.copy(wt_shared[:], weight_bank[0][:, gpsimd_rows])

        def group_offsets(b):
            return offsets[:, b * LIST_COLS : (b + 1) * LIST_COLS]

        w_listed = [held([P, PACK * N], BF16, "w_listed%d" % b) for b in range(B)]
        room = [[1, 2, 0, 1], [0, 1, 2, 3]]

        def plane(b, j, count=1):
            return w_listed[b][:, room[b][j] * N : (room[b][j] + count) * N]
        w_by_d = [held([P, N * PACK], BF16, "w_by_d%d" % b) for b in range(B)]

        def gather_plane(j, b):
            nc.vector.tensor_copy(plane(b, j), table[j][:].indirect(group_offsets(b)))

        def gather_shared(j, slots):
            cut = LIST_COLS + slots // 16
            nc.vector.tensor_copy(plane(1, j)[:, :slots], table[j][:].indirect(offsets[:, LIST_COLS:cut]))
            nc.scalar.activation(plane(1, j)[:, slots:], table[j][:].indirect(offsets[:, cut:]), ACT.Copy)

        def weave_w(b, planes, copy, places=slice(0, PACK)):
            copy(
                w_by_d[b][:].rearrange("p (t c i j) -> p c t i j", t=PACK, i=2, j=PACK)[:, :, places, :, planes],
                plane(b, planes.start, 2).rearrange("p (j c i t) -> p c t i j", j=2, i=2, t=PACK)[:, :, places],
            )

        def turn(b, j, bank, half):
            words = plane(b, j).bitcast(F32)
            for u in range(2):
                nc.tensor.transpose(bank[:, (2 * half + u) * P : (2 * half + u + 1) * P], words[:, u : N // 2 : 2], identity[:])

        def lay(bank, groups, planes, halves_of_bank=slice(0, 2)):
            by_slot = w_by_slot[:].bitcast(F32).rearrange("p (b h j m u) -> p b j h m u", b=B, h=2, j=PACK, u=2)
            nc.scalar.copy(
                by_slot[:, groups, planes],
                bank[:].rearrange("p (k u h m) -> p k h m u", k=2, u=2, h=2)[:, halves_of_bank],
            )

        for b in range(B):
            gather_plane(0, b)

        ts_listed = held([P, B * N], F32, "ts_listed")
        nc.vector.tensor_copy(ts_listed[:, :N], ts_row[:].indirect(group_offsets(0)))
        nc.scalar.activation(ts_listed[:, N:], ts_row[:].indirect(group_offsets(1)), ACT.Copy)
        gather_plane(1, 0)
        gather_shared(1, N // 2)
        for b in range(B):
            nc.gpsimd.tensor_scalar(
                w_by_d[b][:].rearrange("p (t m j) -> p t m j", t=PACK, j=PACK)[:, :, :, 0:2],
                plane(b, 0, 2).rearrange("p (j m t) -> p t m j", j=2, t=PACK),
                1.0,
                0.0,
                ALU.mult,
                ALU.add,
            )

        ts_read = held([P, 2, B, PACK], F32, "ts_read")
        ts_made = held([P, 2, B, PACK], F32, "ts_made")
        ts_col = [ts_read[:, 0, b, :] for b in range(B)]
        ts_abs = [ts_read[:, 1, b, :] for b in range(B)]
        ts_square = [ts_made[:, 0, b, :] for b in range(B)]
        ts_minus_abs = [ts_made[:, 1, b, :] for b in range(B)]
        for b in range(B):
            turned = place_bank[b][:].rearrange("p (t m) -> p t m", t=PACK)
            for t in range(PACK):
                nc.tensor.transpose(turned[:, t, :], ts_listed[:, b * N + t : (b + 1) * N : PACK], identity[:])
            nc.scalar.copy(ts_col[b], turned[:, :, P - 1])
            nc.scalar.activation(ts_abs[b], turned[:, :, P - 1], ACT.Abs)
            nc.scalar.activation(ts_square[b], turned[:, :, P - 1], ACT.Square)
            nc.scalar.activation(ts_minus_abs[b], ts_abs[b], ACT.Copy, scale=-1.0)

        def packed(width, pool, name, tag=None):
            codes = pool.tile([P, width], U32, name=name + "_codes", tag=tag or name + "_codes", align_bytes=64)
            scales = pool.tile([P, width], U8, name=name + "_scales", align_bytes=64)
            return codes, scales

        def quantize(operand, columns, values, fmt):
            nc.vector.quantize_mx(out=operand[0][:, columns].bitcast(fmt), scales=operand[1][:, columns], in_=values)

        def quantized(values, width, fmt, pool, name, tag=None):
            operand = packed(width, pool, name, tag)
            quantize(operand, slice(0, width), values, fmt)
            return operand

        def multiply(bank, stationary, m_cols, fmt, moving, n_cols):
            nc.tensor.matmul_mx(
                out=bank,
                lhsT=stationary[0][:, m_cols].bitcast(fmt),
                lhsT_scale=stationary[1][:, m_cols],
                rhs=moving[0][:, n_cols].bitcast(E4M3),
                rhs_scale=moving[1][:, n_cols],
                start=True,
                stop=True,
            )

        def load_y(b, rows, tag):
            y_raw = held([P, 2, N], F32, "y_raw%d_%d" % (b, rows.start), tag)
            nc.sync.dma_start(y_raw[:], y[b, rows, :].rearrange("(p c) n -> p c n", c=2))
            return [y_raw[:, c, :] for c in range(2)]

        def load_x(b, rows, tag):
            x_raw = held([P, PACK, rows.stop - rows.start], F32, "x_raw%d_%d" % (b, rows.start), tag)
            nc.sync.dma_start(x_raw[:], xT[b].rearrange("(p j) r -> p j r", j=PACK)[:, :, rows])
            return x_raw

        def weave_x(x_by_d, x_raw, rows, copy):
            quads = slice(rows.start // QUAD, rows.stop // QUAD)
            copy(
                x_by_d[:].rearrange("p (c i j) -> p c j i", i=QUAD, j=PACK)[:, quads],
                x_raw.rearrange("p j (c i) -> p c j i", i=QUAD),
            )

        def scale_out(target, b, t, bank):
            nc.scalar.activation(
                target.rearrange("p (h m c) -> p h m c", h=2, c=2),
                bank[:].rearrange("p (h c m) -> p h m c", h=2, c=2),
                ACT.Copy,
                scale=ts_col[b][:, t : t + 1],
            )
            return target

        def scaled_targets(target, b, t, y_raw, bank):
            turned = bank[:].rearrange("p (c m) -> p c m", c=PACK)
            for c in range(PACK):
                nc.tensor.transpose(turned[:, c, :], y_raw[c][:, t:N:PACK], identity[:])
            return scale_out(target, b, t, bank)

        def clip(b, t, residual, clipped, rows):
            engine = nc.gpsimd if t < GPSIMD_PLACES else nc.vector
            engine.tensor_scalar(
                clipped[:, t, rows],
                residual[:, rows],
                ts_abs[b][:, t : t + 1],
                ts_minus_abs[b][:, t : t + 1],
                ALU.min,
                ALU.max,
            )

        def scores(w_q, x_q, banks):
            for t in range(PACK):
                multiply(banks[t][:], w_q, slice(t * P, (t + 1) * P), E4M3, x_q, all_rows)

        def residuals(b, targets, banks):
            clipped = held([P, PACK, R], F32, "clipped%d" % b)
            residual = []
            for t in range(PACK):
                residual.append(ring.tile([P, R], F32, name="residual"))
                nc.vector.scalar_tensor_tensor(
                    residual[t][:], banks[t][:], ts_square[b][:, t : t + 1], targets[t], ALU.mult, ALU.subtract
                )
                if t >= 1:
                    clip(b, t - 1, residual[t - 1], clipped, all_rows)
            return clipped, residual[LAST]

        def h_tile(count):
            return ring.tile([P, count * PACK], BF16, name="h", align_bytes=64)

        def weigh(h, b, rows, clipped):
            count = rows.stop - rows.start
            weights = weight_bank[b][:, rows].rearrange("p (c i) -> p c i", i=QUAD)
            nc.vector.tensor_tensor(
                h.rearrange("p (c i t) -> p c t i", i=QUAD, t=PACK),
                clipped[:, :, rows].rearrange("p t (c i) -> p c t i", i=QUAD),
                weights.unsqueeze(2).to_broadcast([P, count // QUAD, PACK, QUAD]),
                ALU.mult,
            )

        def finish(b, rows, h, h_q, w_slot_q, banks):
            count = rows.stop - rows.start
            parts = 2 if (b, rows.stop) == (B - 1, R) else 1
            for i in range(parts):
                columns = slice(i * count // parts, (i + 1) * count // parts)
                quantize(h_q, columns, h[:, columns.start * PACK : columns.stop * PACK], E5M2)
            for k in range(rows.start // P, rows.stop // P):
                tile_rows = slice(k * P - rows.start, (k + 1) * P - rows.start)
                result = held([P, D], F32, "result%d_%d" % (b, k))
                if (b, k) == (B - 1, LAST):
                    shares = [(banks[k], nc.vector.tensor_copy), (result_bank[0], nc.scalar.copy)]
                else:
                    shares = [(banks[k], nc.scalar.copy)]
                width = D // len(shares)
                for i, (bank, copy) in enumerate(shares):
                    start = b * D + i * width
                    multiply(bank[:, :width], h_q, tile_rows, E5M2, w_slot_q, slice(start, start + width))
                    d_cols = slice(i * width, (i + 1) * width)
                    copy(
                        result[:, d_cols].rearrange("p (h m j) -> p h m j", m=P // 2, j=PACK),
                        bank[:, :width].rearrange("p (h j m) -> p h m j", j=PACK, m=P // 2),
                    )
                    nc.sync.dma_start(out[b, k * P : (k + 1) * P, d_cols], result[:, d_cols])

        all_rows = slice(0, R)
        halves = [slice(0, R // 2), slice(R // 2, R)]

        w_by_slot = held([P, B * D * PACK], BF16, "w_by_slot")
        for b in range(B):
            for j in range(2):
                turn(b, j, result_bank[b], j)
            lay(result_bank[b], b, slice(0, 2))
        spread_weights(1)
        gather_plane(2, 0)
        gather_shared(2, N // 2)
        for b in range(B):
            turn(b, 2, result_bank[b], 0)
        gather_plane(LAST, 0)
        gather_shared(LAST, VECTOR_SLOTS)
        for places in (slice(0, 2), slice(2, PACK)):
            weave_w(0, slice(2, PACK), nc.vector.tensor_copy, places)
        weave_w(1, slice(2, PACK), nc.scalar.copy)

        y_raw0 = load_y(0, halves[0], None)
        x_raw0 = load_x(0, all_rows, "x0_last")
        pairs_of_rows = y[0, halves[1], :].rearrange("(p c) n -> p c n", c=2)
        for c, tag in enumerate((None, "y0_last")):
            y_raw0.append(held([P, N], F32, "y_raw0_late%d" % c, tag))
            nc.sync.dma_start(y_raw0[-1][:], pairs_of_rows[:, c, :])
        x_raw1 = placed.tile([P, PACK, R], F32, name="x_raw1", offset=6144, align_bytes=64)
        nc.sync.dma_start(x_raw1[:], xT[1].rearrange("(p j) r -> p j r", j=PACK))
        y_raw1 = load_y(1, halves[0], None) + load_y(1, halves[1], None)

        w_q0 = packed(N, keep, "w_q")
        for slots in halves:
            quantize(w_q0, slots, w_by_d[0][:, slots.start * PACK : slots.stop * PACK], E4M3)
        x_by_d0 = held([P, R * PACK], BF16, "x_by_d0")
        for rows in halves:
            weave_x(x_by_d0, x_raw0[:, :, rows], rows, nc.vector.tensor_copy)
        def turn_y0(tiles, places):
            for c in tiles:
                for t in places:
                    nc.tensor.transpose(place_bank[t][:, c * P : (c + 1) * P], y_raw0[c][:, t:N:PACK], identity[:])

        turn_y0(range(2), range(PACK))
        for b in range(B):
            turn(b, LAST, result_bank[b], 1)
            lay(result_bank[b], b, slice(2, PACK))
        for t in range(PACK):
            turn_y0(range(2, ROW_TILES), [t])
        early = held([P, PACK, R], F32, "targets0")
        targets0 = [early[:, t, :] for t in range(PACK)]
        for t in range(PACK):
            scale_out(targets0[t], 0, t, place_bank[t])
        x_q0 = packed(R, keep, "x_q")
        for rows in halves:
            quantize(x_q0, rows, x_by_d0[:, rows.start * PACK : rows.stop * PACK], E4M3)
        w_slot_q = quantized(w_by_slot[:], B * D, E4M3, keep, "w_slot_q", "x0_last")
        score_banks0 = result_bank + place_bank[:2]
        scores(w_q0, x_q0, score_banks0)
        clipped0, residual0 = residuals(0, targets0, score_banks0)
        w_q1 = quantized(w_by_d[1][:], N, E4M3, keep, "w_q")
        clip(0, LAST, residual0, clipped0, all_rows)

        x_by_d1 = held([P, R * PACK], BF16, "x_by_d1", "y0_last")
        weave_x(x_by_d1, x_raw1[:], all_rows, nc.scalar.copy)
        y_banks1 = place_bank[2:] + result_bank
        late = placed.tile([P, PACK, R], F32, name="targets1", offset=0, align_bytes=64)
        targets1 = [scaled_targets(late[:, t, :], 1, t, y_raw1, y_banks1[t]) for t in range(PACK)]
        x_q1 = quantized(x_by_d1[:], R, E4M3, keep, "x_q")
        score_banks1 = place_bank
        scores(w_q1, x_q1, score_banks1)

        h_first = placed.tile([P, R // 2 * PACK], BF16, name="h_first", offset=8192, align_bytes=64)
        weigh(h_first[:], 0, halves[0], clipped0)
        h_second = held([P, R // 2 * PACK], BF16, "h_second", "y0_last")
        h_cut = (gpsimd_rows.start - R // 2) * PACK
        nc.gpsimd.tensor_tensor(
            h_second[:, h_cut:].rearrange("p (c i t) -> p c t i", i=QUAD, t=PACK),
            clipped0[:, :, gpsimd_rows].rearrange("p t (c i) -> p c t i", i=QUAD),
            wt_shared[:].rearrange("p (c i) -> p c i", i=QUAD).unsqueeze(2).to_broadcast([P, GPSIMD_ROWS // QUAD, PACK, QUAD]),
            ALU.mult,
        )
        weigh(h_second[:, :h_cut], 0, slice(R // 2, gpsimd_rows.start), clipped0)
        result_banks0 = result_bank + result_bank
        finish(0, halves[0], h_first, packed(R // 2, ring, "h"), w_slot_q, result_banks0)

        clipped1, residual1 = residuals(1, targets1, score_banks1)
        late_codes = placed.tile([P, R // 2], U32, name="late_codes", offset=6144, align_bytes=64)
        late_scales = held([P, R // 2], U8, "late_scales")
        finish(0, halves[1], h_second, (late_codes, late_scales), w_slot_q, result_banks0)
        for rows in halves:
            clip(1, LAST, residual1, clipped1, rows)

        row_tiles = [slice(r, r + P) for r in range(0, R, P)]
        hs = [held([P, P * PACK], BF16, "h1_%d" % k) for k in range(LAST)]
        for k in range(LAST):
            weigh(hs[k][:], 1, row_tiles[k], clipped1)
            if k >= 1:
                finish(1, row_tiles[k - 1], hs[k - 1], packed(P, ring, "h"), w_slot_q, score_banks1)
        finish(1, row_tiles[LAST - 1], hs[LAST - 1], packed(P, ring, "h"), w_slot_q, score_banks1)
        h_last = held([P, P * PACK], BF16, "h_last", "h1_1")
        for i in range(2):
            rows = slice(R - P + i * P // 2, R - P + (i + 1) * P // 2)
            weigh(h_last[:, i * P * 2 : (i + 1) * P * 2], 1, rows, clipped1)
        finish(1, row_tiles[LAST], h_last, packed(P, ring, "h"), w_slot_q, score_banks1)
